import numpy as np
import ml_dtypes


def mxq(x, axis, fmt="e4m3"):
    dtype, down = {"e4m3": (ml_dtypes.float8_e4m3fn, 7), "e5m2": (ml_dtypes.float8_e5m2, 14)}[fmt]
    v = np.moveaxis(np.asarray(x, np.float32).astype(ml_dtypes.bfloat16).astype(np.float64), axis, -1)
    blocks = v.reshape(v.shape[:-1] + (-1, 32))
    amax = np.abs(blocks).max(-1, keepdims=True)
    byte = np.maximum(np.where(amax > 0, np.frexp(amax)[1] - 1 + 127, 0) - down, 1)
    scale = np.exp2(byte - 127.0)
    codes = (blocks / scale).astype(np.float32).astype(dtype).astype(np.float64)
    return np.moveaxis((codes * scale).reshape(v.shape), -1, axis)


WIDE = False


def mx_kscale(k):
    if not WIDE:
        return np.ones(k)
    levels = np.array([10, -10, 5, -5, 0])
    if k % 512:
        return np.exp2(np.random.permutation(np.resize(levels, k // 32))).repeat(32)
    a = np.empty((k // 512, 16))
    for p in range(k // 512):
        a[p, :8] = np.random.permutation(np.resize(levels, 8))
        for g in range(8):
            far = levels[np.abs(levels - a[p, g]) >= 10]
            a[p, g + 8] = far[np.random.randint(len(far))]
    return np.exp2(a.ravel()).repeat(32)


def f64(x):
    return np.asarray(x).astype(np.float64)


def striped(idx):
    return np.tile(idx.reshape(-1, 16).T, (8, 1)).astype(np.uint16)


def unstriped(offs):
    return offs[:16].T.reshape(-1).astype(np.int64)


E2M1 = np.array([0.0, 0.5, 1.0, 1.5, 2.0, 3.0, 4.0, 6.0, -0.0, -0.5, -1.0, -1.5, -2.0, -3.0, -4.0, -6.0])


def pack_weight(w, fmt):
    k, n = w.shape
    w = f64(np.asarray(w, np.float32).astype(ml_dtypes.bfloat16)).reshape(k // 32, 32, n)
    amax = np.abs(w).max(1)
    if fmt == "e4m3":
        byte = np.frexp(amax)[1] - 1 + 127 - 7
    else:
        mant, ex = np.frexp(amax / 6.0)
        byte = np.where(mant > 0.5, ex, ex - 1) + 127
    byte = np.clip(np.where(amax > 0, byte, 1), 1, 254)
    scaled = (w * np.exp2(127.0 - byte)[:, None, :]).reshape(k, n).astype(np.float32)
    by_word = np.ascontiguousarray(scaled.reshape(k // 512, 128, 4, n).transpose(0, 1, 3, 2))
    if fmt == "e4m3":
        words = by_word.astype(ml_dtypes.float8_e4m3fn).view(np.uint8)
    else:
        c = by_word.astype(ml_dtypes.float4_e2m1fn).view(np.uint8) & 0xF
        words = (c[..., 0::2] | (c[..., 1::2] << 4)).reshape(k // 512, 128, 2 * n)
    return np.ascontiguousarray(words), np.ascontiguousarray(byte.astype(np.uint8).reshape(k // 512, 16, n))


def unpack_weight(words, scales, fmt):
    g, _, n = scales.shape
    words = np.ascontiguousarray(words).reshape(g, 128, n, -1)
    if fmt == "e4m3":
        vals = words.view(ml_dtypes.float8_e4m3fn).astype(np.float64)
    else:
        nib = np.empty((g, 128, n, 4), np.uint8)
        nib[..., 0::2] = words & 0xF
        nib[..., 1::2] = words >> 4
        vals = E2M1[nib]
    vals = vals * np.repeat(np.exp2(scales.astype(np.float64) - 127.0), 8, axis=1)[..., None]
    return vals.transpose(0, 1, 3, 2).reshape(g * 512, n)


def gelu(v):
    return 0.5 * v * (1.0 + np.tanh(np.sqrt(2.0 / np.pi) * (v + 0.044715 * v**3)))


def striped8(idx):
    return np.concatenate([v.reshape(-1, 16).T for v in idx]).astype(np.uint16)


def unstriped8(offs):
    return np.stack([offs[16 * g:16 * g + 16].T.reshape(-1) for g in range(8)]).astype(np.int64)


def heads(h, wgt, idx8):
    r = np.arange(h.shape[0])
    return wgt[r // 4 % 128] * h[r[:, None], idx8[r % 512 // 64]]


K, T, S, H, P, N = 1024, 2048, 1024, 1024, 512, 512

def setup_inputs():
    n = np.random.standard_normal
    s = mx_kscale(K)[:, None]
    u = mx_kscale(H)[:, None]
    tab_words, tab_scales = pack_weight(n((K, T)) * s, "e4m3")
    w1_words, w1_scales = pack_weight(0.6 * n((K, H)) / np.sqrt(K) / s, "e2m1")
    w4_words, w4_scales = pack_weight(1.5 * n((H, N)) / np.sqrt(H) / u, "e4m3")
    return {
        "tab_words": tab_words, "tab_scales": tab_scales,
        "offs": striped(np.random.permutation(T)[:S]),
        "offs2": striped8(np.stack([np.random.permutation(S)[:P] for _ in range(8)])),
        "w1_words": w1_words, "w1_scales": w1_scales,
        "w2": (0.6 * n((K, H)) / np.sqrt(K) / s).astype(np.float32),
        "wgt": np.repeat(np.random.uniform(0.5, 2.0, (8, P)), 16, axis=0).astype(np.float32),
        "gain": (np.random.uniform(0.5, 1.5, H) * u[:, 0]).astype(np.float32),
        "w4_words": w4_words, "w4_scales": w4_scales,
        "w5": (0.8 * n((K, N)) / np.sqrt(K) / s).astype(np.float32),
        "prompts": (n((K, P)) * s).astype(np.float32),
        "bias": (0.4 * n(N)).astype(np.float32),
    }

def reference(tab_words, tab_scales, offs, offs2, w1_words, w1_scales, w2, wgt, gain,
              w4_words, w4_scales, w5, prompts, bias):
    v = unpack_weight(tab_words, tab_scales, "e4m3")[:, unstriped(offs)]
    w1 = unpack_weight(w1_words, w1_scales, "e2m1")
    w4 = unpack_weight(w4_words, w4_scales, "e4m3")
    h = (w1.T @ v) - (mxq(f64(w2), 0, "e4m3").T @ v)
    x = heads(h, f64(wgt), unstriped8(offs2))
    z = np.tanh(x) * f64(gain)[:, None]
    y = (w4.T @ mxq(z, 0, "e4m3")
              + mxq(f64(w5), 0, "e4m3").T @ mxq(f64(prompts), 0, "e4m3"))
    return np.abs(y + f64(bias)[:, None])

@@ -1,0 +1,278 @@
+from contextlib import ExitStack
+
+import concourse.mybir as mybir
+
+K, T, S, H, M, N = 1024, 2048, 1024, 1024, 512, 512
+FLOPS = 2 * 2 * K * H * S + 2 * (H + K) * N * M
+
+F32 = mybir.dt.float32
+BF16 = mybir.dt.bfloat16
+I32 = mybir.dt.int32
+U32 = mybir.dt.uint32
+U16 = mybir.dt.uint16
+U8 = mybir.dt.uint8
+FP8X4 = mybir.dt.float8_e4m3fn_x4
+FP4X4 = mybir.dt.float4_e2m1fn_x4
+ACT = mybir.ActivationFunctionType
+ALU = mybir.AluOpType
+
+P = 128
+W = 512
+
+
+def tile_list_judge_disagreement_audit_kernel(
+    tc, tab_words, tab_scales, offs, offs2, w1_words, w1_scales, w2, wgt, gain,
+    w4_words, w4_scales, w5, prompts, bias, out,
+):
+    nc = tc.nc
+    with ExitStack() as ctx:
+        keep = ctx.enter_context(tc.tile_pool(name="keep", bufs=1))
+        psum = ctx.enter_context(tc.psum_pool(name="psum", bufs=1))
+
+        def kept(shape, dtype, name):
+            return keep.tile(shape, dtype, name=name, align_bytes=64)
+
+        def staged(shape, dtype, name, slot):
+            return keep.tile(shape, dtype, name=name, tag=slot, align_bytes=64)
+
+        def zero(plane):
+            nc.vector.memset(plane[:].bitcast(I32), 0)
+
+        def load_scale_rows(plane, first, scales):
+            for q in range(4):
+                nc.sync.dma_start(
+                    out=plane[32 * q + first : 32 * q + first + 8, :].bitcast(I32),
+                    in_=scales[:, 4 * q : 4 * q + 4, :].bitcast(I32),
+                )
+
+        idx = keep.tile([P, S // 16], U16, name="idx")
+        idx2 = keep.tile([P, M // 16], U16, name="idx2")
+        tab_plane = staged([P, T], U8, "tab_plane", "big0")
+        w1_plane_raw = staged([P, 2 * H], U8, "w1_plane_raw", "w1_scales")
+        v_rows = staged([P, S], U8, "v_rows", "v_rows")
+        v_plane = [kept([P, S], U8, "v_plane%d" % a) for a in range(2)]
+        w1_plane = kept([P, 2 * H], U8, "w1_plane")
+        w1_sb = [kept([P, 2, 2 * W], U8, "w1_sb%d" % b) for b in range(2)]
+        warm = kept([P, 1], F32, "warm")
+
+        nc.gpsimd.memset(w1_plane_raw[:].bitcast(I32), 0)
+        for q in range(4):
+            nc.vector.memset(tab_plane[32 * q : 32 * q + 24, :].bitcast(I32), 0)
+        for plane in v_plane:
+            nc.gpsimd.memset(plane[:].bitcast(I32), 0)
+        nc.vector.memset(warm[:], 0.0)
+        nc.scalar.activation(out=warm[:], in_=warm[:], func=ACT.Tanh)
+
+        tab_sb = {}
+        w1_raw = {}
+
+        def load_table(a, slot):
+            tab_sb[a] = staged([P, T], I32, "tab_sb", slot)
+            nc.sync.dma_start(out=tab_sb[a][:], in_=tab_words[a].rearrange("p t i -> p (t i)").bitcast(I32))
+
+        def load_w1(b):
+            w1_raw[b] = staged([P, 2, W // 2], I32, "w1_raw", "w1_words")
+            nc.sync.dma_start(
+                out=w1_raw[b][:],
+                in_=w1_words.bitcast(I32)[:, :, W // 2 * b : W // 2 * (b + 1)].rearrange("a p c -> p a c"),
+            )
+
+        def load_rows(src, a, cols, slot):
+            raw = staged([P, 4, W], F32, "raw", slot)
+            nc.sync.dma_start(out=raw[:], in_=src[W * a : W * (a + 1), cols].rearrange("(p j) c -> p j c", j=4))
+            return raw
+
+        load_scale_rows(tab_plane, 24, tab_scales)
+        nc.sync.dma_start(idx[:], offs)
+        load_table(0, "big1")
+        load_w1(0)
+        nc.sync.dma_start(idx2[:], offs2)
+        w2_raw = {}
+        w2_raw[0, 0] = load_rows(w2, 0, slice(0, W), "big2")
+        for q in range(4):
+            nc.sync.dma_start(
+                out=w1_plane_raw[32 * q : 32 * q + 4, :].bitcast(I32).rearrange("r (a c) -> r a c", a=2),
+                in_=w1_scales[:, 4 * q : 4 * q + 4, :].bitcast(I32).rearrange("a r c -> r a c"),
+            )
+        nc.vector.tensor_copy(v_rows[:], tab_plane[:].indirect(idx[:]))
+        for a in range(2):
+            nc.scalar.dma_start(
+                out=v_plane[a][0:100, :].bitcast(I32), in_=v_rows[24 + 4 * a : 124 + 4 * a, :].bitcast(I32)
+            )
+        load_table(1, "big0")
+        w4_plane = staged([P, N], U8, "w4_plane", "v_rows")
+        zero(w4_plane)
+        load_scale_rows(w4_plane, 0, w4_scales)
+
+        def order_w1_words(b):
+            nc.vector.tensor_copy(
+                out=w1_sb[b][:].bitcast(U16).rearrange("p a (t m) -> p a t m", t=4),
+                in_=w1_raw[b][:].bitcast(U16).rearrange("p a (m t) -> p a t m", t=4),
+            )
+
+        def order_w1_scales():
+            nc.vector.tensor_copy(
+                out=w1_plane[:].rearrange("p (g t m) -> p g t m", t=4, m=P),
+                in_=w1_plane_raw[:].rearrange("p (g m t) -> p g t m", t=4, m=P),
+            )
+
+        v_words = {}
+
+        def gather_words(a):
+            for c in range(2):
+                v_words[a, c] = kept([P, W], U32, "v_words%d%d" % (a, c))
+                nc.vector.tensor_copy(
+                    v_words[a, c][:], tab_sb[a][:].bitcast(U32).indirect(idx[:, 32 * c : 32 * (c + 1)])
+                )
+
+        gather_words(0)
+        w2_raw[0, 1] = load_rows(w2, 1, slice(0, W), "big1")
+        order_w1_words(0)
+        load_w1(1)
+        order_w1_scales()
+
+        def quantize(rounded, name, width=W, slot=None):
+            codes = staged([P, width], U32, name + "_codes", slot or name + "_codes")
+            plane = kept([P, width], U8, name + "_plane")
+            nc.vector.quantize_mx(out=codes[:].bitcast(FP8X4), scales=plane[:], in_=rounded[:])
+            return codes, plane
+
+        def round_w2(b, a, scalar_share, slot):
+            rounded = staged([P, 4 * W], BF16, "w2_rounded", slot)
+            dst = rounded[:].rearrange("p (t m j) -> p m j t", t=4, j=4)
+            src = w2_raw[b, a][:].rearrange("p j (m t) -> p m j t", t=4)
+            if scalar_share > 0:
+                part = slice(0, scalar_share)
+                nc.scalar.activation(out=dst[:, part], in_=src[:, part], func=ACT.Copy, scale=-1.0)
+            if scalar_share < P:
+                part = slice(scalar_share, P)
+                nc.vector.tensor_scalar(out=dst[:, part], in0=src[:, part], scalar1=-1.0, scalar2=None, op0=ALU.mult)
+            return rounded
+
+        def round_plain(raw, on_scalar, slot):
+            rounded = staged([P, 4 * W], BF16, "rounded", slot)
+            dst = rounded[:].rearrange("p (c i j) -> p c j i", i=4, j=4)
+            src = raw[:].rearrange("p j (c i) -> p c j i", i=4)
+            if on_scalar:
+                nc.scalar.activation(out=dst, in_=src, func=ACT.Copy)
+            else:
+                nc.vector.tensor_copy(out=dst, in_=src)
+            return rounded
+
+        w2_q = {}
+        x = [kept([P, 4, M], F32, "x%d" % b) for b in range(2)]
+
+        def scores(b, t, parts=1):
+            h = staged([P, S], F32, "h", "h%d%d" % (b, t))
+            for c in range(2):
+                acc = psum.tile([P, W], F32, name="acc", tag="bank%d" % (2 * (0, 1, 0, 1, 2, 0, 1, 2)[4 * b + t] + c))
+                cols = slice(W * c, W * (c + 1))
+
+                def w1_pass(a, start, stop):
+                    nc.tensor.matmul_mx(
+                        out=acc[:],
+                        lhsT=w1_sb[b][:, a, 2 * P * t : 2 * P * (t + 1)].bitcast(FP4X4),
+                        lhsT_scale=w1_plane[:, H * a + W * b + P * t : H * a + W * b + P * (t + 1)],
+                        rhs=v_words[a, c][:].bitcast(FP8X4),
+                        rhs_scale=v_plane[a][:, cols],
+                        start=start, stop=stop,
+                    )
+
+                def w2_pass(a, start, stop):
+                    codes, plane = w2_q[b, a]
+                    nc.tensor.matmul_mx(
+                        out=acc[:],
+                        lhsT=codes[:, P * t : P * (t + 1)].bitcast(FP8X4),
+                        lhsT_scale=plane[:, P * t : P * (t + 1)],
+                        rhs=v_words[a, c][:].bitcast(FP8X4),
+                        rhs_scale=v_plane[a][:, cols],
+                        start=start, stop=stop,
+                    )
+
+                w1_pass(0, True, False)
+                w2_pass(0, False, False)
+                w1_pass(1, False, False)
+                w2_pass(1, False, True)
+                nc.scalar.copy(out=h[:, cols], in_=acc[:])
+            width = M // parts
+            for u in range(parts):
+                cols = slice(width * u, width * (u + 1))
+                picks = idx2[:, width // 16 * u : width // 16 * (u + 1)]
+                nc.vector.tensor_tensor(x[b][:, t, cols], h[:].indirect(picks), wgt_sb[:, cols], ALU.mult)
+                nc.scalar.activation(out=x[b][:, t, cols], in_=x[b][:, t, cols], func=ACT.Tanh)
+
+        def bounded(b, cols, name):
+            width = cols.stop - cols.start
+            rounded = kept([P, 4 * width], BF16, name)
+            nc.vector.tensor_tensor(
+                rounded[:].rearrange("p (c i t) -> p c t i", i=4, t=4),
+                x[b][:, :, cols].rearrange("p t (c i) -> p c t i", i=4),
+                gain_sb[:, b, :].unsqueeze(1).unsqueeze(3).broadcast_to([P, width // 4, 4, 4]),
+                ALU.mult,
+            )
+            return quantize(rounded, name, width)
+
+        w5_raw, pr_raw = {}, {}
+        w2_q[0, 0] = quantize(round_w2(0, 0, P, "r00"), "w2_00", slot="w1_scales")
+        w2_raw[1, 0] = load_rows(w2, 0, slice(W, 2 * W), "big2")
+        wgt_sb = staged([P, M], F32, "wgt_sb", "r00")
+        nc.sync.dma_start(out=wgt_sb[:], in_=wgt)
+        gather_words(1)
+        pass
+        w2_raw[1, 1] = load_rows(w2, 1, slice(W, 2 * W), "big0")
+        w2_q[0, 1] = quantize(round_w2(0, 1, 96, "r01"), "w2_01")
+        w5_raw[0] = load_rows(w5, 0, slice(0, N), "big1")
+        order_w1_words(1)
+        pr_raw[0] = load_rows(prompts, 0, slice(0, M), "w1_words")
+        gain_sb = staged([P, 2, 4], F32, "gain_sb", "r01")
+        nc.sync.dma_start(out=gain_sb[:], in_=gain.rearrange("(b p t) -> p b t", b=2, t=4))
+        w2_q[1, 0] = quantize(round_w2(1, 0, P, "r10"), "w2_10")
+        w5_raw[1] = load_rows(w5, 1, slice(0, N), "big2")
+        pr_raw[1] = load_rows(prompts, 1, slice(0, M), "r10")
+        scores(0, 0)
+        w2_q[1, 1] = quantize(round_w2(1, 1, 0, "h00"), "w2_11")
+        w4_sb = staged([P, 2, N], I32, "w4_sb", "big0")
+        nc.sync.dma_start(out=w4_sb[:], in_=w4_words.rearrange("a p c i -> p a (c i)").bitcast(I32))
+        bias_sb = staged([P, N // P], F32, "bias_sb", "h00")
+        with nc.allow_non_contiguous_dma(reason="one bias value for each output row"):
+            nc.sync.dma_start(out=bias_sb[:], in_=bias.rearrange("(j p) -> p j", p=P))
+        for t in range(1, 4):
+            scores(0, t)
+        w5_q, pr_q = {}, {}
+        scores(1, 0)
+        z0 = bounded(0, slice(0, M), "z0")
+        w5_q[0] = quantize(round_plain(w5_raw[0], True, "h03"), "w5_0")
+        scores(1, 1)
+        pr_q[0] = quantize(round_plain(pr_raw[0], True, "h10"), "pr_0")
+        scores(1, 2)
+        w5_q[1] = quantize(round_plain(w5_raw[1], True, "h11"), "w5_1")
+        scores(1, 3, 2)
+        pr_q[1] = quantize(round_plain(pr_raw[1], True, "h12"), "pr_1")
+
+        half = M // 2
+        for u in range(2):
+            cols = slice(half * u, half * (u + 1))
+            z1 = bounded(1, cols, "z1%d" % u)
+            result = kept([P, N // P, half], F32, "result%d" % u)
+            flags = [psum.tile([P, half], F32, name="flags", tag="bank%d" % ((6, 7, 0, 1), (2, 3, 4, 5))[u][j]) for j in range(N // P)]
+
+            def add_pass(j, codes, plane, rhs, rhs_plane, start, stop):
+                nc.tensor.matmul_mx(
+                    out=flags[j][:], lhsT=codes.bitcast(FP8X4), lhsT_scale=plane,
+                    rhs=rhs.bitcast(FP8X4), rhs_scale=rhs_plane, start=start, stop=stop,
+                )
+
+            for j in range(N // P):
+                rows = slice(P * j, P * (j + 1))
+                for a in range(2):
+                    add_pass(j, w5_q[a][0][:, rows], w5_q[a][1][:, rows], pr_q[a][0][:, cols], pr_q[a][1][:, cols], a == 0, False)
+                add_pass(j, w4_sb[:, 0, rows], w4_plane[:, rows], z0[0][:, cols], z0[1][:, cols], False, False)
+            for j in range(N // P):
+                rows = slice(P * j, P * (j + 1))
+                add_pass(j, w4_sb[:, 1, rows], w4_plane[4:P, rows], z1[0][:], z1[1][:], False, True)
+                nc.scalar.activation(out=result[:, j, :], in_=flags[j][:], func=ACT.Abs, bias=bias_sb[:, j : j + 1])
+                if j % 2 == 1:
+                    nc.sync.dma_start(
+                        out=out[P * (j - 1) : P * (j + 1), cols].rearrange("(j p) m -> p j m", p=P),
+                        in_=result[:, j - 1 : j + 1, :],
+                    )

@@ -100,9 +100,6 @@ def tile_list_judge_disagreement_audit_kernel(
                 out=v_plane[a][0:100, :].bitcast(I32), in_=v_rows[24 + 4 * a : 124 + 4 * a, :].bitcast(I32)
             )
         load_table(1, "big0")
-        w4_plane = staged([P, N], U8, "w4_plane", "v_rows")
-        zero(w4_plane)
-        load_scale_rows(w4_plane, 0, w4_scales)
 
         def order_w1_words(b):
             nc.vector.tensor_copy(
@@ -149,15 +146,13 @@ def tile_list_judge_disagreement_audit_kernel(
                 nc.vector.tensor_scalar(out=dst[:, part], in0=src[:, part], scalar1=-1.0, scalar2=None, op0=ALU.mult)
             return rounded
 
-        def round_plain(raw, on_scalar, slot):
-            rounded = staged([P, 4 * W], BF16, "rounded", slot)
+        def round_plain(raw, scalar_share, name):
+            rounded = kept([P, 4 * W], BF16, name + "_rounded")
             dst = rounded[:].rearrange("p (c i j) -> p c j i", i=4, j=4)
             src = raw[:].rearrange("p j (c i) -> p c j i", i=4)
-            if on_scalar:
-                nc.scalar.activation(out=dst, in_=src, func=ACT.Copy)
-            else:
-                nc.vector.tensor_copy(out=dst, in_=src)
-            return rounded
+            nc.scalar.activation(out=dst[:, :scalar_share], in_=src[:, :scalar_share], func=ACT.Copy)
+            nc.vector.tensor_copy(out=dst[:, scalar_share:], in_=src[:, scalar_share:])
+            return quantize(rounded, name)
 
         w2_q = {}
         x = [kept([P, 4, M], F32, "x%d" % b) for b in range(2)]
@@ -165,7 +160,7 @@ def tile_list_judge_disagreement_audit_kernel(
         def scores(b, t, parts=1):
             h = staged([P, S], F32, "h", "h%d%d" % (b, t))
             for c in range(2):
-                acc = psum.tile([P, W], F32, name="acc", tag="bank%d" % (2 * (0, 1, 0, 1, 2, 0, 1, 2)[4 * b + t] + c))
+                acc = psum.tile([P, W], F32, name="acc", tag="bank%d" % (2 * ((4 * b + t) % 3) + c))
                 cols = slice(W * c, W * (c + 1))
 
                 def w1_pass(a, start, stop):
@@ -199,7 +194,9 @@ def tile_list_judge_disagreement_audit_kernel(
                 cols = slice(width * u, width * (u + 1))
                 picks = idx2[:, width // 16 * u : width // 16 * (u + 1)]
                 nc.vector.tensor_tensor(x[b][:, t, cols], h[:].indirect(picks), wgt_sb[:, cols], ALU.mult)
-                nc.scalar.activation(out=x[b][:, t, cols], in_=x[b][:, t, cols], func=ACT.Tanh)
+
+        def bound(b, slices, cols):
+            nc.scalar.activation(out=x[b][:, slices, cols], in_=x[b][:, slices, cols], func=ACT.Tanh)
 
         def bounded(b, cols, name):
             width = cols.stop - cols.start
@@ -220,41 +217,51 @@ def tile_list_judge_disagreement_audit_kernel(
         gather_words(1)
         pass
         w2_raw[1, 1] = load_rows(w2, 1, slice(W, 2 * W), "big0")
-        w2_q[0, 1] = quantize(round_w2(0, 1, 96, "r01"), "w2_01")
+        w2_q[0, 1] = quantize(round_w2(0, 1, 80, "r01"), "w2_01")
         w5_raw[0] = load_rows(w5, 0, slice(0, N), "big1")
         order_w1_words(1)
         pr_raw[0] = load_rows(prompts, 0, slice(0, M), "w1_words")
         gain_sb = staged([P, 2, 4], F32, "gain_sb", "r01")
         nc.sync.dma_start(out=gain_sb[:], in_=gain.rearrange("(b p t) -> p b t", b=2, t=4))
-        w2_q[1, 0] = quantize(round_w2(1, 0, P, "r10"), "w2_10")
+        w4_plane = staged([P, N], U8, "w4_plane", "v_rows")
+        zero(w4_plane)
+        load_scale_rows(w4_plane, 0, w4_scales)
+        scores(0, 0)
+        w2_q[1, 0] = quantize(round_w2(1, 0, 0, "r10"), "w2_10")
         w5_raw[1] = load_rows(w5, 1, slice(0, N), "big2")
         pr_raw[1] = load_rows(prompts, 1, slice(0, M), "r10")
-        scores(0, 0)
-        w2_q[1, 1] = quantize(round_w2(1, 1, 0, "h00"), "w2_11")
+        scores(0, 1)
+        w2_q[1, 1] = quantize(round_w2(1, 1, 64, "r11"), "w2_11")
         w4_sb = staged([P, 2, N], I32, "w4_sb", "big0")
         nc.sync.dma_start(out=w4_sb[:], in_=w4_words.rearrange("a p c i -> p a (c i)").bitcast(I32))
-        bias_sb = staged([P, N // P], F32, "bias_sb", "h00")
+        bias_sb = staged([P, N // P], F32, "bias_sb", "r11")
         with nc.allow_non_contiguous_dma(reason="one bias value for each output row"):
             nc.sync.dma_start(out=bias_sb[:], in_=bias.rearrange("(j p) -> p j", p=P))
-        for t in range(1, 4):
-            scores(0, t)
-        w5_q, pr_q = {}, {}
-        scores(1, 0)
-        z0 = bounded(0, slice(0, M), "z0")
-        w5_q[0] = quantize(round_plain(w5_raw[0], True, "h03"), "w5_0")
-        scores(1, 1)
-        pr_q[0] = quantize(round_plain(pr_raw[0], True, "h10"), "pr_0")
-        scores(1, 2)
-        w5_q[1] = quantize(round_plain(w5_raw[1], True, "h11"), "w5_1")
+        scores(0, 2)
+        scores(0, 3)
+        for t in range(3):
+            scores(1, t)
         scores(1, 3, 2)
-        pr_q[1] = quantize(round_plain(pr_raw[1], True, "h12"), "pr_1")
+        every = slice(0, M)
+        w5_q, pr_q = {}, {}
+        bound(0, slice(0, 2), every)
+        bound(0, slice(2, 4), every)
+        z0 = bounded(0, every, "z0")
+        pr_q[0] = round_plain(pr_raw[0], 64, "pr_0")
+        w5_q[0] = round_plain(w5_raw[0], 64, "w5_0")
+        bound(1, slice(0, 2), every)
+        w5_q[1] = round_plain(w5_raw[1], 64, "w5_1")
+        pr_q[1] = round_plain(pr_raw[1], 64, "pr_1")
+        bound(1, slice(2, 3), every)
+        bound(1, slice(3, 4), slice(0, M // 2))
+        bound(1, slice(3, 4), slice(M // 2, M))
 
         half = M // 2
         for u in range(2):
             cols = slice(half * u, half * (u + 1))
             z1 = bounded(1, cols, "z1%d" % u)
             result = kept([P, N // P, half], F32, "result%d" % u)
-            flags = [psum.tile([P, half], F32, name="flags", tag="bank%d" % ((6, 7, 0, 1), (2, 3, 4, 5))[u][j]) for j in range(N // P)]
+            flags = [psum.tile([P, half], F32, name="flags", tag="bank%d" % (7 - j if u == 0 else j)) for j in range(N // P)]
 
             def add_pass(j, codes, plane, rhs, rhs_plane, start, stop):
                 nc.tensor.matmul_mx(
@@ -271,8 +278,4 @@ def tile_list_judge_disagreement_audit_kernel(
                 rows = slice(P * j, P * (j + 1))
                 add_pass(j, w4_sb[:, 1, rows], w4_plane[4:P, rows], z1[0][:], z1[1][:], False, True)
                 nc.scalar.activation(out=result[:, j, :], in_=flags[j][:], func=ACT.Abs, bias=bias_sb[:, j : j + 1])
-                if j % 2 == 1:
-                    nc.sync.dma_start(
-                        out=out[P * (j - 1) : P * (j + 1), cols].rearrange("(j p) m -> p j m", p=P),
-                        in_=result[:, j - 1 : j + 1, :],
-                    )
+                nc.sync.dma_start(out=out[rows, cols], in_=result[:, j, :])

@@ -56,8 +56,7 @@ def tile_list_judge_disagreement_audit_kernel(
         warm = kept([P, 1], F32, "warm")
 
         nc.gpsimd.memset(w1_plane_raw[:].bitcast(I32), 0)
-        for q in range(4):
-            nc.vector.memset(tab_plane[32 * q : 32 * q + 24, :].bitcast(I32), 0)
+        nc.vector.memset(tab_plane[0:96, :].bitcast(I32), 0)
         for plane in v_plane:
             nc.gpsimd.memset(plane[:].bitcast(I32), 0)
         nc.vector.memset(warm[:], 0.0)
@@ -82,7 +81,7 @@ def tile_list_judge_disagreement_audit_kernel(
             nc.sync.dma_start(out=raw[:], in_=src[W * a : W * (a + 1), cols].rearrange("(p j) c -> p j c", j=4))
             return raw
 
-        load_scale_rows(tab_plane, 24, tab_scales)
+        nc.sync.dma_start(out=tab_plane[96:P, :].bitcast(I32), in_=tab_scales.rearrange("a q t -> (a q) t").bitcast(I32))
         nc.sync.dma_start(idx[:], offs)
         load_table(0, "big1")
         load_w1(0)
@@ -95,11 +94,16 @@ def tile_list_judge_disagreement_audit_kernel(
                 in_=w1_scales[:, 4 * q : 4 * q + 4, :].bitcast(I32).rearrange("a r c -> r a c"),
             )
         nc.vector.tensor_copy(v_rows[:], tab_plane[:].indirect(idx[:]))
-        for a in range(2):
-            nc.scalar.dma_start(
-                out=v_plane[a][0:100, :].bitcast(I32), in_=v_rows[24 + 4 * a : 124 + 4 * a, :].bitcast(I32)
-            )
+
+        def place_scale_rows(a):
+            for q in range(4):
+                first = 96 + 16 * a + 4 * q
+                nc.sync.dma_start(
+                    out=v_plane[a][32 * q : 32 * q + 4, :].bitcast(I32), in_=v_rows[first : first + 4, :].bitcast(I32)
+                )
+
         load_table(1, "big0")
+        place_scale_rows(0)
 
         def order_w1_words(b):
             nc.vector.tensor_copy(
@@ -124,6 +128,7 @@ def tile_list_judge_disagreement_audit_kernel(
 
         gather_words(0)
         w2_raw[0, 1] = load_rows(w2, 1, slice(0, W), "big1")
+        place_scale_rows(1)
         order_w1_words(0)
         load_w1(1)
         order_w1_scales()
@@ -150,8 +155,10 @@ def tile_list_judge_disagreement_audit_kernel(
             rounded = kept([P, 4 * W], BF16, name + "_rounded")
             dst = rounded[:].rearrange("p (c i j) -> p c j i", i=4, j=4)
             src = raw[:].rearrange("p j (c i) -> p c j i", i=4)
-            nc.scalar.activation(out=dst[:, :scalar_share], in_=src[:, :scalar_share], func=ACT.Copy)
-            nc.vector.tensor_copy(out=dst[:, scalar_share:], in_=src[:, scalar_share:])
+            if scalar_share > 0:
+                nc.scalar.activation(out=dst[:, :scalar_share], in_=src[:, :scalar_share], func=ACT.Copy)
+            if scalar_share < P:
+                nc.vector.tensor_copy(out=dst[:, scalar_share:], in_=src[:, scalar_share:])
             return quantize(rounded, name)
 
         w2_q = {}
@@ -196,14 +203,14 @@ def tile_list_judge_disagreement_audit_kernel(
                 nc.vector.tensor_tensor(x[b][:, t, cols], h[:].indirect(picks), wgt_sb[:, cols], ALU.mult)
 
         def bound(b, slices, cols):
-            nc.scalar.activation(out=x[b][:, slices, cols], in_=x[b][:, slices, cols], func=ACT.Tanh)
+            nc.scalar.activation(out=y[b][:, slices, cols], in_=x[b][:, slices, cols], func=ACT.Tanh)
 
         def bounded(b, cols, name):
             width = cols.stop - cols.start
             rounded = kept([P, 4 * width], BF16, name)
             nc.vector.tensor_tensor(
                 rounded[:].rearrange("p (c i t) -> p c t i", i=4, t=4),
-                x[b][:, :, cols].rearrange("p t (c i) -> p c t i", i=4),
+                y[b][:, :, cols].rearrange("p t (c i) -> p c t i", i=4),
                 gain_sb[:, b, :].unsqueeze(1).unsqueeze(3).broadcast_to([P, width // 4, 4, 4]),
                 ALU.mult,
             )
@@ -215,7 +222,6 @@ def tile_list_judge_disagreement_audit_kernel(
         wgt_sb = staged([P, M], F32, "wgt_sb", "r00")
         nc.sync.dma_start(out=wgt_sb[:], in_=wgt)
         gather_words(1)
-        pass
         w2_raw[1, 1] = load_rows(w2, 1, slice(W, 2 * W), "big0")
         w2_q[0, 1] = quantize(round_w2(0, 1, 80, "r01"), "w2_01")
         w5_raw[0] = load_rows(w5, 0, slice(0, N), "big1")
@@ -244,14 +250,16 @@ def tile_list_judge_disagreement_audit_kernel(
         scores(1, 3, 2)
         every = slice(0, M)
         w5_q, pr_q = {}, {}
+        y = {0: x[0]}
         bound(0, slice(0, 2), every)
         bound(0, slice(2, 4), every)
         z0 = bounded(0, every, "z0")
-        pr_q[0] = round_plain(pr_raw[0], 64, "pr_0")
+        pr_q[0] = round_plain(pr_raw[0], 0, "pr_0")
         w5_q[0] = round_plain(w5_raw[0], 64, "w5_0")
+        w5_q[1] = round_plain(w5_raw[1], P, "w5_1")
+        pr_q[1] = round_plain(pr_raw[1], P, "pr_1")
+        y[1] = staged([P, 4, M], F32, "y1", "r10")
         bound(1, slice(0, 2), every)
-        w5_q[1] = round_plain(w5_raw[1], 64, "w5_1")
-        pr_q[1] = round_plain(pr_raw[1], 64, "pr_1")
         bound(1, slice(2, 3), every)
         bound(1, slice(3, 4), slice(0, M // 2))
         bound(1, slice(3, 4), slice(M // 2, M))
@@ -271,9 +279,9 @@ def tile_list_judge_disagreement_audit_kernel(
 
             for j in range(N // P):
                 rows = slice(P * j, P * (j + 1))
+                add_pass(j, w4_sb[:, 0, rows], w4_plane[:, rows], z0[0][:, cols], z0[1][:, cols], True, False)
                 for a in range(2):
-                    add_pass(j, w5_q[a][0][:, rows], w5_q[a][1][:, rows], pr_q[a][0][:, cols], pr_q[a][1][:, cols], a == 0, False)
-                add_pass(j, w4_sb[:, 0, rows], w4_plane[:, rows], z0[0][:, cols], z0[1][:, cols], False, False)
+                    add_pass(j, w5_q[a][0][:, rows], w5_q[a][1][:, rows], pr_q[a][0][:, cols], pr_q[a][1][:, cols], False, False)
             for j in range(N // P):
                 rows = slice(P * j, P * (j + 1))
                 add_pass(j, w4_sb[:, 1, rows], w4_plane[4:P, rows], z1[0][:], z1[1][:], False, True)

@@ -35,9 +35,6 @@ def tile_list_judge_disagreement_audit_kernel(
         def staged(shape, dtype, name, slot):
             return keep.tile(shape, dtype, name=name, tag=slot, align_bytes=64)
 
-        def zero(plane):
-            nc.vector.memset(plane[:].bitcast(I32), 0)
-
         def load_scale_rows(plane, first, scales):
             for q in range(4):
                 nc.sync.dma_start(
@@ -47,11 +44,10 @@ def tile_list_judge_disagreement_audit_kernel(
 
         idx = keep.tile([P, S // 16], U16, name="idx")
         idx2 = keep.tile([P, M // 16], U16, name="idx2")
-        tab_plane = staged([P, T], U8, "tab_plane", "big0")
-        w1_plane_raw = staged([P, 2 * H], U8, "w1_plane_raw", "w1_scales")
-        v_rows = staged([P, S], U8, "v_rows", "v_rows")
+        tab_plane = kept([P, T], U8, "tab_plane")
+        w1_plane_raw = kept([P, 2 * H], U8, "w1_plane_raw")
+        v_rows = kept([P, S], U8, "v_rows")
         v_plane = [kept([P, S], U8, "v_plane%d" % a) for a in range(2)]
-        w1_plane = kept([P, 2 * H], U8, "w1_plane")
         w1_sb = [kept([P, 2, 2 * W], U8, "w1_sb%d" % b) for b in range(2)]
         warm = kept([P, 1], F32, "warm")
 
@@ -62,15 +58,16 @@ def tile_list_judge_disagreement_audit_kernel(
         nc.vector.memset(warm[:], 0.0)
         nc.scalar.activation(out=warm[:], in_=warm[:], func=ACT.Tanh)
 
-        tab_sb = {}
-        w1_raw = {}
+        tab_sb, w1_raw, w1_plane, v_words = {}, {}, {}, {}
+        w2_raw, w2_q, w5_raw, w5_q, pr_raw, pr_q = {}, {}, {}, {}, {}, {}
+        acc, h, x, y = {}, {}, {}, {}
 
         def load_table(a, slot):
             tab_sb[a] = staged([P, T], I32, "tab_sb", slot)
             nc.sync.dma_start(out=tab_sb[a][:], in_=tab_words[a].rearrange("p t i -> p (t i)").bitcast(I32))
 
         def load_w1(b):
-            w1_raw[b] = staged([P, 2, W // 2], I32, "w1_raw", "w1_words")
+            w1_raw[b] = kept([P, 2, W // 2], I32, "w1_raw%d" % b)
             nc.sync.dma_start(
                 out=w1_raw[b][:],
                 in_=w1_words.bitcast(I32)[:, :, W // 2 * b : W // 2 * (b + 1)].rearrange("a p c -> p a c"),
@@ -81,20 +78,6 @@ def tile_list_judge_disagreement_audit_kernel(
             nc.sync.dma_start(out=raw[:], in_=src[W * a : W * (a + 1), cols].rearrange("(p j) c -> p j c", j=4))
             return raw
 
-        nc.sync.dma_start(out=tab_plane[96:P, :].bitcast(I32), in_=tab_scales.rearrange("a q t -> (a q) t").bitcast(I32))
-        nc.sync.dma_start(idx[:], offs)
-        load_table(0, "big1")
-        load_w1(0)
-        nc.sync.dma_start(idx2[:], offs2)
-        w2_raw = {}
-        w2_raw[0, 0] = load_rows(w2, 0, slice(0, W), "big2")
-        for q in range(4):
-            nc.sync.dma_start(
-                out=w1_plane_raw[32 * q : 32 * q + 4, :].bitcast(I32).rearrange("r (a c) -> r a c", a=2),
-                in_=w1_scales[:, 4 * q : 4 * q + 4, :].bitcast(I32).rearrange("a r c -> r a c"),
-            )
-        nc.vector.tensor_copy(v_rows[:], tab_plane[:].indirect(idx[:]))
-
         def place_scale_rows(a):
             for q in range(4):
                 first = 96 + 16 * a + 4 * q
@@ -102,22 +85,16 @@ def tile_list_judge_disagreement_audit_kernel(
                     out=v_plane[a][32 * q : 32 * q + 4, :].bitcast(I32), in_=v_rows[first : first + 4, :].bitcast(I32)
                 )
 
-        load_table(1, "big0")
-        place_scale_rows(0)
-
-        def order_w1_words(b):
+        def order_w1(b, slot):
             nc.vector.tensor_copy(
                 out=w1_sb[b][:].bitcast(U16).rearrange("p a (t m) -> p a t m", t=4),
                 in_=w1_raw[b][:].bitcast(U16).rearrange("p a (m t) -> p a t m", t=4),
             )
-
-        def order_w1_scales():
+            w1_plane[b] = staged([P, 2, W], U8, "w1_plane", slot)
             nc.vector.tensor_copy(
-                out=w1_plane[:].rearrange("p (g t m) -> p g t m", t=4, m=P),
-                in_=w1_plane_raw[:].rearrange("p (g m t) -> p g t m", t=4, m=P),
+                out=w1_plane[b][:].rearrange("p a (t m) -> p a t m", t=4),
+                in_=w1_plane_raw[:].rearrange("p (a b m t) -> p b a t m", a=2, b=2, t=4)[:, b],
             )
-
-        v_words = {}
 
         def gather_words(a):
             for c in range(2):
@@ -125,13 +102,6 @@ def tile_list_judge_disagreement_audit_kernel(
                 nc.vector.tensor_copy(
                     v_words[a, c][:], tab_sb[a][:].bitcast(U32).indirect(idx[:, 32 * c : 32 * (c + 1)])
                 )
-
-        gather_words(0)
-        w2_raw[0, 1] = load_rows(w2, 1, slice(0, W), "big1")
-        place_scale_rows(1)
-        order_w1_words(0)
-        load_w1(1)
-        order_w1_scales()
 
         def quantize(rounded, name, width=W, slot=None):
             codes = staged([P, width], U32, name + "_codes", slot or name + "_codes")
@@ -151,139 +121,170 @@ def tile_list_judge_disagreement_audit_kernel(
                 nc.vector.tensor_scalar(out=dst[:, part], in0=src[:, part], scalar1=-1.0, scalar2=None, op0=ALU.mult)
             return rounded
 
-        def round_plain(raw, scalar_share, name):
-            rounded = kept([P, 4 * W], BF16, name + "_rounded")
+        def round_plain(raw, scalar_share, slot):
+            rounded = staged([P, 4 * W], BF16, "rounded", slot)
             dst = rounded[:].rearrange("p (c i j) -> p c j i", i=4, j=4)
             src = raw[:].rearrange("p j (c i) -> p c j i", i=4)
             if scalar_share > 0:
                 nc.scalar.activation(out=dst[:, :scalar_share], in_=src[:, :scalar_share], func=ACT.Copy)
             if scalar_share < P:
                 nc.vector.tensor_copy(out=dst[:, scalar_share:], in_=src[:, scalar_share:])
-            return quantize(rounded, name)
+            return rounded
 
-        w2_q = {}
-        x = [kept([P, 4, M], F32, "x%d" % b) for b in range(2)]
+        def score_pass(b, t, c, weight, a, start=False, stop=False):
+            if start:
+                acc[b, t, c] = psum.tile([P, W], F32, name="acc", tag="bank%d" % (2 * t + c))
+            cols = slice(W * c, W * (c + 1))
+            if weight == 1:
+                lhs = w1_sb[b][:, a, 2 * P * t : 2 * P * (t + 1)].bitcast(FP4X4)
+                lhs_plane = w1_plane[b][:, a, P * t : P * (t + 1)]
+            else:
+                lhs = w2_q[b, a][0][:, P * t : P * (t + 1)].bitcast(FP8X4)
+                lhs_plane = w2_q[b, a][1][:, P * t : P * (t + 1)]
+            nc.tensor.matmul_mx(
+                out=acc[b, t, c][:], lhsT=lhs, lhsT_scale=lhs_plane,
+                rhs=v_words[a, c][:].bitcast(FP8X4), rhs_scale=v_plane[a][:, cols], start=start, stop=stop,
+            )
 
-        def scores(b, t, parts=1):
-            h = staged([P, S], F32, "h", "h%d%d" % (b, t))
+        def sweep(b, weight, a, start=False):
             for c in range(2):
-                acc = psum.tile([P, W], F32, name="acc", tag="bank%d" % (2 * ((4 * b + t) % 3) + c))
-                cols = slice(W * c, W * (c + 1))
+                for t in range(4):
+                    score_pass(b, t, c, weight, a, start=start)
 
-                def w1_pass(a, start, stop):
-                    nc.tensor.matmul_mx(
-                        out=acc[:],
-                        lhsT=w1_sb[b][:, a, 2 * P * t : 2 * P * (t + 1)].bitcast(FP4X4),
-                        lhsT_scale=w1_plane[:, H * a + W * b + P * t : H * a + W * b + P * (t + 1)],
-                        rhs=v_words[a, c][:].bitcast(FP8X4),
-                        rhs_scale=v_plane[a][:, cols],
-                        start=start, stop=stop,
-                    )
+        def close(b, t, a):
+            h[b, t] = staged([P, S], F32, "h", "h%d%d" % (b, t))
+            for c in range(2):
+                score_pass(b, t, c, 2, a, stop=True)
+                nc.scalar.copy(out=h[b, t][:, W * c : W * (c + 1)], in_=acc[b, t, c][:])
 
-                def w2_pass(a, start, stop):
-                    codes, plane = w2_q[b, a]
-                    nc.tensor.matmul_mx(
-                        out=acc[:],
-                        lhsT=codes[:, P * t : P * (t + 1)].bitcast(FP8X4),
-                        lhsT_scale=plane[:, P * t : P * (t + 1)],
-                        rhs=v_words[a, c][:].bitcast(FP8X4),
-                        rhs_scale=v_plane[a][:, cols],
-                        start=start, stop=stop,
-                    )
-
-                w1_pass(0, True, False)
-                w2_pass(0, False, False)
-                w1_pass(1, False, False)
-                w2_pass(1, False, True)
-                nc.scalar.copy(out=h[:, cols], in_=acc[:])
+        def pick(b, t, parts=1):
             width = M // parts
             for u in range(parts):
                 cols = slice(width * u, width * (u + 1))
                 picks = idx2[:, width // 16 * u : width // 16 * (u + 1)]
-                nc.vector.tensor_tensor(x[b][:, t, cols], h[:].indirect(picks), wgt_sb[:, cols], ALU.mult)
+                nc.vector.tensor_tensor(x[b][:, t, cols], h[b, t][:].indirect(picks), wgt_sb[:, cols], ALU.mult)
 
         def bound(b, slices, cols):
             nc.scalar.activation(out=y[b][:, slices, cols], in_=x[b][:, slices, cols], func=ACT.Tanh)
 
-        def bounded(b, cols, name):
+        def with_gain(b, cols, slot):
             width = cols.stop - cols.start
-            rounded = kept([P, 4 * width], BF16, name)
+            rounded = staged([P, 4 * width], BF16, "z_rounded", slot)
             nc.vector.tensor_tensor(
                 rounded[:].rearrange("p (c i t) -> p c t i", i=4, t=4),
                 y[b][:, :, cols].rearrange("p t (c i) -> p c t i", i=4),
                 gain_sb[:, b, :].unsqueeze(1).unsqueeze(3).broadcast_to([P, width // 4, 4, 4]),
                 ALU.mult,
             )
-            return quantize(rounded, name, width)
+            return rounded
 
-        w5_raw, pr_raw = {}, {}
-        w2_q[0, 0] = quantize(round_w2(0, 0, P, "r00"), "w2_00", slot="w1_scales")
-        w2_raw[1, 0] = load_rows(w2, 0, slice(W, 2 * W), "big2")
-        wgt_sb = staged([P, M], F32, "wgt_sb", "r00")
+        nc.sync.dma_start(out=tab_plane[96:P, :].bitcast(I32), in_=tab_scales.rearrange("a q t -> (a q) t").bitcast(I32))
+        nc.sync.dma_start(idx[:], offs)
+        load_w1(0)
+        for q in range(4):
+            nc.sync.dma_start(
+                out=w1_plane_raw[32 * q : 32 * q + 4, :].bitcast(I32).rearrange("r (a c) -> r a c", a=2),
+                in_=w1_scales[:, 4 * q : 4 * q + 4, :].bitcast(I32).rearrange("a r c -> r a c"),
+            )
+        load_table(0, "big0")
+        w2_raw[0, 0] = load_rows(w2, 0, slice(0, W), "big1")
+        nc.vector.tensor_copy(v_rows[:], tab_plane[:].indirect(idx[:]))
+        place_scale_rows(0)
+        load_table(1, "big2")
+        place_scale_rows(1)
+        w2_raw[0, 1] = load_rows(w2, 1, slice(0, W), "big3")
+        load_w1(1)
+        w2_raw[1, 0] = load_rows(w2, 0, slice(W, 2 * W), "big4")
+        w2_raw[1, 1] = load_rows(w2, 1, slice(W, 2 * W), "big5")
+        wgt_sb = kept([P, M], F32, "wgt_sb")
         nc.sync.dma_start(out=wgt_sb[:], in_=wgt)
+        nc.sync.dma_start(idx2[:], offs2)
+
+        order_w1(0, "w1_plane0")
+        gather_words(0)
+        sweep(0, 1, 0, start=True)
+        w2_q[0, 0] = quantize(round_w2(0, 0, 80, "r00"), "w2_00")
+        sweep(0, 2, 0)
         gather_words(1)
-        w2_raw[1, 1] = load_rows(w2, 1, slice(W, 2 * W), "big0")
-        w2_q[0, 1] = quantize(round_w2(0, 1, 80, "r01"), "w2_01")
-        w5_raw[0] = load_rows(w5, 0, slice(0, N), "big1")
-        order_w1_words(1)
-        pr_raw[0] = load_rows(prompts, 0, slice(0, M), "w1_words")
-        gain_sb = staged([P, 2, 4], F32, "gain_sb", "r01")
+        order_w1(1, "big2")
+        w2_q[0, 1] = quantize(round_w2(0, 1, 96, "r01"), "w2_01")
+
+        w5_raw[0] = load_rows(w5, 0, slice(0, N), "big0")
+        pr_raw[0] = load_rows(prompts, 0, slice(0, M), "big1")
+        gain_sb = kept([P, 2, 4], F32, "gain_sb")
         nc.sync.dma_start(out=gain_sb[:], in_=gain.rearrange("(b p t) -> p b t", b=2, t=4))
-        w4_plane = staged([P, N], U8, "w4_plane", "v_rows")
-        zero(w4_plane)
-        load_scale_rows(w4_plane, 0, w4_scales)
-        scores(0, 0)
-        w2_q[1, 0] = quantize(round_w2(1, 0, 0, "r10"), "w2_10")
-        w5_raw[1] = load_rows(w5, 1, slice(0, N), "big2")
-        pr_raw[1] = load_rows(prompts, 1, slice(0, M), "r10")
-        scores(0, 1)
-        w2_q[1, 1] = quantize(round_w2(1, 1, 64, "r11"), "w2_11")
-        w4_sb = staged([P, 2, N], I32, "w4_sb", "big0")
+        w5_raw[1] = load_rows(w5, 1, slice(0, N), "big4")
+        pr_raw[1] = load_rows(prompts, 1, slice(0, M), "big3")
+        w4_sb = kept([P, 2, N], I32, "w4_sb")
         nc.sync.dma_start(out=w4_sb[:], in_=w4_words.rearrange("a p c i -> p a (c i)").bitcast(I32))
-        bias_sb = staged([P, N // P], F32, "bias_sb", "r11")
+        w4_plane = kept([P, N], U8, "w4_plane")
+        nc.gpsimd.memset(w4_plane[:].bitcast(I32), 0)
+        load_scale_rows(w4_plane, 0, w4_scales)
+        bias_sb = kept([P, N // P], F32, "bias_sb")
         with nc.allow_non_contiguous_dma(reason="one bias value for each output row"):
             nc.sync.dma_start(out=bias_sb[:], in_=bias.rearrange("(j p) -> p j", p=P))
-        scores(0, 2)
-        scores(0, 3)
-        for t in range(3):
-            scores(1, t)
-        scores(1, 3, 2)
+
+        for t in range(4):
+            for c in range(2):
+                score_pass(0, t, c, 1, 1)
+            close(0, t, 1)
+        w2_q[1, 0] = quantize(round_w2(1, 0, 0, "r10"), "w2_10")
+        w2_q[1, 1] = quantize(round_w2(1, 1, 0, "r11"), "w2_11")
+        x[0] = staged([P, 4, M], F32, "x0", "r11")
+        x[1] = kept([P, 4, M], F32, "x1")
+        for t in range(4):
+            pick(0, t)
+        for t in range(4):
+            for c in range(2):
+                score_pass(1, t, c, 2, 1, start=True)
+                score_pass(1, t, c, 1, 0)
+                score_pass(1, t, c, 1, 1)
+            close(1, t, 0)
         every = slice(0, M)
-        w5_q, pr_q = {}, {}
-        y = {0: x[0]}
+        w5_q[0] = quantize(round_plain(w5_raw[0], P, "r00"), "w5_0")
+        pr_q[0] = quantize(round_plain(pr_raw[0], P, "r10"), "pr_0")
+        y[0] = staged([P, 4, M], F32, "y0", "big0")
         bound(0, slice(0, 2), every)
         bound(0, slice(2, 4), every)
-        z0 = bounded(0, every, "z0")
-        pr_q[0] = round_plain(pr_raw[0], 0, "pr_0")
-        w5_q[0] = round_plain(w5_raw[0], 64, "w5_0")
-        w5_q[1] = round_plain(w5_raw[1], P, "w5_1")
-        pr_q[1] = round_plain(pr_raw[1], P, "pr_1")
-        y[1] = staged([P, 4, M], F32, "y1", "r10")
+        for t in range(3):
+            pick(1, t)
+        pick(1, 3, 2)
+        w5_q[1] = quantize(round_plain(w5_raw[1], P, "h00"), "w5_1")
+        pr_q[1] = quantize(round_plain(pr_raw[1], 0, "h01"), "pr_1")
+        y[1] = staged([P, 4, M], F32, "y1", "big4")
         bound(1, slice(0, 2), every)
         bound(1, slice(2, 3), every)
         bound(1, slice(3, 4), slice(0, M // 2))
         bound(1, slice(3, 4), slice(M // 2, M))
-
         half = M // 2
-        for u in range(2):
-            cols = slice(half * u, half * (u + 1))
-            z1 = bounded(1, cols, "z1%d" % u)
+        halves = [slice(0, half), slice(half, M)]
+        blocks = [slice(P * j, P * (j + 1)) for j in range(N // P)]
+        flags = {}
+
+        def add_pass(u, j, codes, plane, rhs, rhs_plane, start=False, stop=False):
+            if start:
+                flags[u, j] = psum.tile([P, half], F32, name="flags", tag="bank%d" % (4 * u + j))
+            nc.tensor.matmul_mx(
+                out=flags[u, j][:], lhsT=codes.bitcast(FP8X4), lhsT_scale=plane,
+                rhs=rhs.bitcast(FP8X4), rhs_scale=rhs_plane, start=start, stop=stop,
+            )
+
+        for a in range(2):
+            for u, cols in enumerate(halves):
+                for j, rows in enumerate(blocks):
+                    add_pass(u, j, w5_q[a][0][:, rows], w5_q[a][1][:, rows], pr_q[a][0][:, cols], pr_q[a][1][:, cols], start=a == 0)
+        z0_rounded = with_gain(0, every, "h13")
+        z1_rounded = with_gain(1, halves[0], "z1")
+        z0 = quantize(z0_rounded, "z0")
+        for u, cols in enumerate(halves):
+            for j, rows in enumerate(blocks):
+                add_pass(u, j, w4_sb[:, 0, rows], w4_plane[:, rows], z0[0][:, cols], z0[1][:, cols])
+        for u, cols in enumerate(halves):
+            if u == 1:
+                z1_rounded = with_gain(1, cols, "z1")
+            z1 = quantize(z1_rounded, "z1%d" % u, half)
             result = kept([P, N // P, half], F32, "result%d" % u)
-            flags = [psum.tile([P, half], F32, name="flags", tag="bank%d" % (7 - j if u == 0 else j)) for j in range(N // P)]
-
-            def add_pass(j, codes, plane, rhs, rhs_plane, start, stop):
-                nc.tensor.matmul_mx(
-                    out=flags[j][:], lhsT=codes.bitcast(FP8X4), lhsT_scale=plane,
-                    rhs=rhs.bitcast(FP8X4), rhs_scale=rhs_plane, start=start, stop=stop,
-                )
-
-            for j in range(N // P):
-                rows = slice(P * j, P * (j + 1))
-                add_pass(j, w4_sb[:, 0, rows], w4_plane[:, rows], z0[0][:, cols], z0[1][:, cols], True, False)
-                for a in range(2):
-                    add_pass(j, w5_q[a][0][:, rows], w5_q[a][1][:, rows], pr_q[a][0][:, cols], pr_q[a][1][:, cols], False, False)
-            for j in range(N // P):
-                rows = slice(P * j, P * (j + 1))
-                add_pass(j, w4_sb[:, 1, rows], w4_plane[4:P, rows], z1[0][:], z1[1][:], False, True)
-                nc.scalar.activation(out=result[:, j, :], in_=flags[j][:], func=ACT.Abs, bias=bias_sb[:, j : j + 1])
+            for j, rows in enumerate(blocks):
+                add_pass(u, j, w4_sb[:, 1, rows], w4_plane[4:P, rows], z1[0][:], z1[1][:], stop=True)
+                nc.scalar.activation(out=result[:, j, :], in_=flags[u, j][:], func=ACT.Abs, bias=bias_sb[:, j : j + 1])
                 nc.sync.dma_start(out=out[rows, cols], in_=result[:, j, :])

@@ -27,12 +27,15 @@ def tile_list_judge_disagreement_audit_kernel(
     nc = tc.nc
     with ExitStack() as ctx:
         keep = ctx.enter_context(tc.tile_pool(name="keep", bufs=1))
+        reuse = ctx.enter_context(tc.tile_pool(name="reuse", bufs=1))
         psum = ctx.enter_context(tc.psum_pool(name="psum", bufs=1))
 
         def kept(shape, dtype, name):
             return keep.tile(shape, dtype, name=name, align_bytes=64)
 
         def staged(shape, dtype, name, slot):
+            if isinstance(slot, int):
+                return reuse.tile(shape, dtype, name=name + str(slot), align_bytes=64, offset=slot)
             return keep.tile(shape, dtype, name=name, tag=slot, align_bytes=64)
 
         def load_scale_rows(plane, first, scales):
@@ -48,7 +51,6 @@ def tile_list_judge_disagreement_audit_kernel(
         w1_plane_raw = kept([P, 2 * H], U8, "w1_plane_raw")
         v_rows = kept([P, S], U8, "v_rows")
         v_plane = [kept([P, S], U8, "v_plane%d" % a) for a in range(2)]
-        w1_sb = [kept([P, 2, 2 * W], U8, "w1_sb%d" % b) for b in range(2)]
         warm = kept([P, 1], F32, "warm")
 
         nc.gpsimd.memset(w1_plane_raw[:].bitcast(I32), 0)
@@ -58,9 +60,10 @@ def tile_list_judge_disagreement_audit_kernel(
         nc.vector.memset(warm[:], 0.0)
         nc.scalar.activation(out=warm[:], in_=warm[:], func=ACT.Tanh)
 
-        tab_sb, w1_raw, w1_plane, v_words = {}, {}, {}, {}
+        tab_sb, w1_raw, w1_sb, w1_plane, v_words = {}, {}, {}, {}, {}
         w2_raw, w2_q, w5_raw, w5_q, pr_raw, pr_q = {}, {}, {}, {}, {}, {}
-        acc, h, x, y = {}, {}, {}, {}
+        acc, h = {}, {}
+        x = [staged([P, 4, M], F32, "x", "x%d" % b) for b in range(2)]
 
         def load_table(a, slot):
             tab_sb[a] = staged([P, T], I32, "tab_sb", slot)
@@ -85,11 +88,14 @@ def tile_list_judge_disagreement_audit_kernel(
                     out=v_plane[a][32 * q : 32 * q + 4, :].bitcast(I32), in_=v_rows[first : first + 4, :].bitcast(I32)
                 )
 
-        def order_w1(b, slot):
+        def order_w1_words(b, slot):
+            w1_sb[b] = staged([P, 2, 2 * W], U8, "w1_sb", slot)
             nc.vector.tensor_copy(
                 out=w1_sb[b][:].bitcast(U16).rearrange("p a (t m) -> p a t m", t=4),
                 in_=w1_raw[b][:].bitcast(U16).rearrange("p a (m t) -> p a t m", t=4),
             )
+
+        def order_w1_scales(b, slot):
             w1_plane[b] = staged([P, 2, W], U8, "w1_plane", slot)
             nc.vector.tensor_copy(
                 out=w1_plane[b][:].rearrange("p a (t m) -> p a t m", t=4),
@@ -104,7 +110,7 @@ def tile_list_judge_disagreement_audit_kernel(
                 )
 
         def quantize(rounded, name, width=W, slot=None):
-            codes = staged([P, width], U32, name + "_codes", slot or name + "_codes")
+            codes = staged([P, width], U32, name, slot or name)
             plane = kept([P, width], U8, name + "_plane")
             nc.vector.quantize_mx(out=codes[:].bitcast(FP8X4), scales=plane[:], in_=rounded[:])
             return codes, plane
@@ -121,14 +127,14 @@ def tile_list_judge_disagreement_audit_kernel(
                 nc.vector.tensor_scalar(out=dst[:, part], in0=src[:, part], scalar1=-1.0, scalar2=None, op0=ALU.mult)
             return rounded
 
-        def round_plain(raw, scalar_share, slot):
-            rounded = staged([P, 4 * W], BF16, "rounded", slot)
+        def round_plain(raw, cols, on_scalar, slot):
+            rounded = staged([P, 4 * (cols.stop - cols.start)], BF16, "rounded", slot)
             dst = rounded[:].rearrange("p (c i j) -> p c j i", i=4, j=4)
-            src = raw[:].rearrange("p j (c i) -> p c j i", i=4)
-            if scalar_share > 0:
-                nc.scalar.activation(out=dst[:, :scalar_share], in_=src[:, :scalar_share], func=ACT.Copy)
-            if scalar_share < P:
-                nc.vector.tensor_copy(out=dst[:, scalar_share:], in_=src[:, scalar_share:])
+            src = raw[:, :, cols].rearrange("p j (c i) -> p c j i", i=4)
+            if on_scalar:
+                nc.scalar.activation(out=dst, in_=src, func=ACT.Copy)
+            else:
+                nc.vector.tensor_copy(out=dst, in_=src)
             return rounded
 
         def score_pass(b, t, c, weight, a, start=False, stop=False):
@@ -151,8 +157,8 @@ def tile_list_judge_disagreement_audit_kernel(
                 for t in range(4):
                     score_pass(b, t, c, weight, a, start=start)
 
-        def close(b, t, a):
-            h[b, t] = staged([P, S], F32, "h", "h%d%d" % (b, t))
+        def close(b, t, a, slot):
+            h[b, t] = staged([P, S], F32, "h", slot)
             for c in range(2):
                 score_pass(b, t, c, 2, a, stop=True)
                 nc.scalar.copy(out=h[b, t][:, W * c : W * (c + 1)], in_=acc[b, t, c][:])
@@ -164,15 +170,15 @@ def tile_list_judge_disagreement_audit_kernel(
                 picks = idx2[:, width // 16 * u : width // 16 * (u + 1)]
                 nc.vector.tensor_tensor(x[b][:, t, cols], h[b, t][:].indirect(picks), wgt_sb[:, cols], ALU.mult)
 
-        def bound(b, slices, cols):
-            nc.scalar.activation(out=y[b][:, slices, cols], in_=x[b][:, slices, cols], func=ACT.Tanh)
+        def bound(dst, b, slices, cols):
+            nc.scalar.activation(out=dst[:, slices, :], in_=x[b][:, slices, cols], func=ACT.Tanh)
 
-        def with_gain(b, cols, slot):
-            width = cols.stop - cols.start
+        def with_gain(b, src, slot):
+            width = src.shape[2]
             rounded = staged([P, 4 * width], BF16, "z_rounded", slot)
             nc.vector.tensor_tensor(
                 rounded[:].rearrange("p (c i t) -> p c t i", i=4, t=4),
-                y[b][:, :, cols].rearrange("p t (c i) -> p c t i", i=4),
+                src[:].rearrange("p t (c i) -> p c t i", i=4),
                 gain_sb[:, b, :].unsqueeze(1).unsqueeze(3).broadcast_to([P, width // 4, 4, 4]),
                 ALU.mult,
             )
@@ -191,30 +197,32 @@ def tile_list_judge_disagreement_audit_kernel(
         nc.vector.tensor_copy(v_rows[:], tab_plane[:].indirect(idx[:]))
         place_scale_rows(0)
         load_table(1, "big2")
-        place_scale_rows(1)
         w2_raw[0, 1] = load_rows(w2, 1, slice(0, W), "big3")
-        load_w1(1)
+        place_scale_rows(1)
         w2_raw[1, 0] = load_rows(w2, 0, slice(W, 2 * W), "big4")
+        load_w1(1)
         w2_raw[1, 1] = load_rows(w2, 1, slice(W, 2 * W), "big5")
         wgt_sb = kept([P, M], F32, "wgt_sb")
         nc.sync.dma_start(out=wgt_sb[:], in_=wgt)
         nc.sync.dma_start(idx2[:], offs2)
 
-        order_w1(0, "w1_plane0")
+        order_w1_words(0, "w1_sb0")
+        order_w1_scales(0, "w1_plane0")
         gather_words(0)
         sweep(0, 1, 0, start=True)
-        w2_q[0, 0] = quantize(round_w2(0, 0, 80, "r00"), "w2_00")
+        rounded = round_w2(0, 0, 80, "r00")
+        order_w1_scales(1, "big0")
+        w2_q[0, 0] = quantize(rounded, "w2_00")
         sweep(0, 2, 0)
         gather_words(1)
-        order_w1(1, "big2")
-        w2_q[0, 1] = quantize(round_w2(0, 1, 96, "r01"), "w2_01")
+        w2_q[0, 1] = quantize(round_w2(0, 1, 64, "r01"), "w2_01")
 
-        w5_raw[0] = load_rows(w5, 0, slice(0, N), "big0")
+        w5_raw[0] = load_rows(w5, 0, slice(0, N), 0)
         pr_raw[0] = load_rows(prompts, 0, slice(0, M), "big1")
+        w5_raw[1] = load_rows(w5, 1, slice(0, N), 8192)
+        pr_raw[1] = load_rows(prompts, 1, slice(0, M), "big4")
         gain_sb = kept([P, 2, 4], F32, "gain_sb")
         nc.sync.dma_start(out=gain_sb[:], in_=gain.rearrange("(b p t) -> p b t", b=2, t=4))
-        w5_raw[1] = load_rows(w5, 1, slice(0, N), "big4")
-        pr_raw[1] = load_rows(prompts, 1, slice(0, M), "big3")
         w4_sb = kept([P, 2, N], I32, "w4_sb")
         nc.sync.dma_start(out=w4_sb[:], in_=w4_words.rearrange("a p c i -> p a (c i)").bitcast(I32))
         w4_plane = kept([P, N], U8, "w4_plane")
@@ -227,38 +235,42 @@ def tile_list_judge_disagreement_audit_kernel(
         for t in range(4):
             for c in range(2):
                 score_pass(0, t, c, 1, 1)
-            close(0, t, 1)
-        w2_q[1, 0] = quantize(round_w2(1, 0, 0, "r10"), "w2_10")
+            close(0, t, 1, "h0%d" % t)
+        rounded = round_w2(1, 0, 0, "r10")
+        order_w1_words(1, "w1_sb1")
+        w2_q[1, 0] = quantize(rounded, "w2_10")
         w2_q[1, 1] = quantize(round_w2(1, 1, 0, "r11"), "w2_11")
-        x[0] = staged([P, 4, M], F32, "x0", "r11")
-        x[1] = kept([P, 4, M], F32, "x1")
         for t in range(4):
             pick(0, t)
-        for t in range(4):
-            for c in range(2):
-                score_pass(1, t, c, 2, 1, start=True)
-                score_pass(1, t, c, 1, 0)
-                score_pass(1, t, c, 1, 1)
-            close(1, t, 0)
-        every = slice(0, M)
-        w5_q[0] = quantize(round_plain(w5_raw[0], P, "r00"), "w5_0")
-        pr_q[0] = quantize(round_plain(pr_raw[0], P, "r10"), "pr_0")
-        y[0] = staged([P, 4, M], F32, "y0", "big0")
-        bound(0, slice(0, 2), every)
-        bound(0, slice(2, 4), every)
-        for t in range(3):
-            pick(1, t)
-        pick(1, 3, 2)
-        w5_q[1] = quantize(round_plain(w5_raw[1], P, "h00"), "w5_1")
-        pr_q[1] = quantize(round_plain(pr_raw[1], 0, "h01"), "pr_1")
-        y[1] = staged([P, 4, M], F32, "y1", "big4")
-        bound(1, slice(0, 2), every)
-        bound(1, slice(2, 3), every)
-        bound(1, slice(3, 4), slice(0, M // 2))
-        bound(1, slice(3, 4), slice(M // 2, M))
         half = M // 2
+        every = slice(0, M)
         halves = [slice(0, half), slice(half, M)]
         blocks = [slice(P * j, P * (j + 1)) for j in range(N // P)]
+        w5_q[0] = quantize(round_plain(w5_raw[0], every, True, "r00"), "w5_0")
+        pr_rounded = round_plain(pr_raw[0], every, False, "r10")
+        y0 = staged([P, 4, M], F32, "y0", "big1")
+        for t in range(4):
+            last = 1 if t < 2 else 0
+            for c in range(2):
+                score_pass(1, t, c, 2, 1 - last, start=True)
+                score_pass(1, t, c, 1, 0)
+                score_pass(1, t, c, 1, 1)
+            close(1, t, last, [0, 4096, "r00", "h13"][t])
+            if t >= 2:
+                bound(y0, 0, slice(2 * t - 4, 2 * t - 2), every)
+        for t in range(3):
+            pick(1, t)
+            if t == 0:
+                pr_q[0] = quantize(pr_rounded, "pr_0")
+        pick(1, 3)
+        w5_q[1] = quantize(round_plain(w5_raw[1], every, True, "w2_11"), "w5_1")
+        y1 = [staged([P, 4, half], F32, "y1", 8192 + 6144 * u) for u in range(2)]
+        pr_rounded, pr_late = {}, {}
+        for u in range(2):
+            for slices in (slice(0, 3), slice(3, 4)):
+                bound(y1[u], 1, slices, halves[u])
+            pr_rounded[u] = round_plain(pr_raw[1], halves[u], True, [8192 + 4096, "x1"][u])
+
         flags = {}
 
         def add_pass(u, j, codes, plane, rhs, rhs_plane, start=False, stop=False):
@@ -269,22 +281,30 @@ def tile_list_judge_disagreement_audit_kernel(
                 rhs=rhs.bitcast(FP8X4), rhs_scale=rhs_plane, start=start, stop=stop,
             )
 
-        for a in range(2):
-            for u, cols in enumerate(halves):
-                for j, rows in enumerate(blocks):
-                    add_pass(u, j, w5_q[a][0][:, rows], w5_q[a][1][:, rows], pr_q[a][0][:, cols], pr_q[a][1][:, cols], start=a == 0)
-        z0_rounded = with_gain(0, every, "h13")
-        z1_rounded = with_gain(1, halves[0], "z1")
-        z0 = quantize(z0_rounded, "z0")
-        for u, cols in enumerate(halves):
+        def late_prompt_passes(u):
             for j, rows in enumerate(blocks):
-                add_pass(u, j, w4_sb[:, 0, rows], w4_plane[:, rows], z0[0][:, cols], z0[1][:, cols])
-        for u, cols in enumerate(halves):
-            if u == 1:
-                z1_rounded = with_gain(1, cols, "z1")
-            z1 = quantize(z1_rounded, "z1%d" % u, half)
+                add_pass(u, j, w5_q[1][0][:, rows], w5_q[1][1][:, rows], pr_late[u][0][:], pr_late[u][1][:])
+
+        def finish(u, z1):
+            cols = halves[u]
             result = kept([P, N // P, half], F32, "result%d" % u)
             for j, rows in enumerate(blocks):
                 add_pass(u, j, w4_sb[:, 1, rows], w4_plane[4:P, rows], z1[0][:], z1[1][:], stop=True)
                 nc.scalar.activation(out=result[:, j, :], in_=flags[u, j][:], func=ACT.Abs, bias=bias_sb[:, j : j + 1])
                 nc.sync.dma_start(out=out[rows, cols], in_=result[:, j, :])
+
+        def z0_passes(u):
+            for j, rows in enumerate(blocks):
+                add_pass(u, j, w4_sb[:, 0, rows], w4_plane[:, rows], z0[0][:, halves[u]], z0[1][:, halves[u]])
+
+        for u, cols in enumerate(halves):
+            for j, rows in enumerate(blocks):
+                add_pass(u, j, w5_q[0][0][:, rows], w5_q[0][1][:, rows], pr_q[0][0][:, cols], pr_q[0][1][:, cols], start=True)
+        z0 = quantize(with_gain(0, y0, "z0_rounded"), "z0")
+        for u in range(2):
+            z0_passes(u)
+        for u in range(2):
+            z1_rounded = with_gain(1, y1[u], "z1%d_rounded" % u)
+            pr_late[u] = quantize(pr_rounded[u], "pr_1%d" % u, half)
+            late_prompt_passes(u)
+            finish(u, quantize(z1_rounded, "z1%d" % u, half))

@@ -170,16 +170,20 @@ def tile_list_judge_disagreement_audit_kernel(
                 picks = idx2[:, width // 16 * u : width // 16 * (u + 1)]
                 nc.vector.tensor_tensor(x[b][:, t, cols], h[b, t][:].indirect(picks), wgt_sb[:, cols], ALU.mult)
 
-        def bound(dst, b, slices, cols):
-            nc.scalar.activation(out=dst[:, slices, :], in_=x[b][:, slices, cols], func=ACT.Tanh)
+        def bound(dst, b, cols):
+            nc.scalar.activation(
+                out=dst.rearrange("p (c i) t -> p c t i", i=4),
+                in_=x[b][:, :, cols].rearrange("p t (c i) -> p c t i", i=4),
+                func=ACT.Tanh,
+            )
 
         def with_gain(b, src, slot):
-            width = src.shape[2]
+            width = src.shape[1]
             rounded = staged([P, 4 * width], BF16, "z_rounded", slot)
             nc.vector.tensor_tensor(
-                rounded[:].rearrange("p (c i t) -> p c t i", i=4, t=4),
-                src[:].rearrange("p t (c i) -> p c t i", i=4),
-                gain_sb[:, b, :].unsqueeze(1).unsqueeze(3).broadcast_to([P, width // 4, 4, 4]),
+                rounded[:].rearrange("p (m t) -> p m t", t=4),
+                src[:],
+                gain_sb[:, b, :].unsqueeze(1).broadcast_to([P, width, 4]),
                 ALU.mult,
             )
             return rounded
@@ -248,7 +252,7 @@ def tile_list_judge_disagreement_audit_kernel(
         blocks = [slice(P * j, P * (j + 1)) for j in range(N // P)]
         w5_q[0] = quantize(round_plain(w5_raw[0], every, True, "r00"), "w5_0")
         pr_rounded = round_plain(pr_raw[0], every, False, "r10")
-        y0 = staged([P, 4, M], F32, "y0", "big1")
+        y0 = staged([P, M, 4], F32, "y0", "big1")
         for t in range(4):
             last = 1 if t < 2 else 0
             for c in range(2):
@@ -257,18 +261,17 @@ def tile_list_judge_disagreement_audit_kernel(
                 score_pass(1, t, c, 1, 1)
             close(1, t, last, [0, 4096, "r00", "h13"][t])
             if t >= 2:
-                bound(y0, 0, slice(2 * t - 4, 2 * t - 2), every)
+                bound(y0[:, halves[t - 2], :], 0, halves[t - 2])
         for t in range(3):
             pick(1, t)
             if t == 0:
                 pr_q[0] = quantize(pr_rounded, "pr_0")
         pick(1, 3)
         w5_q[1] = quantize(round_plain(w5_raw[1], every, True, "w2_11"), "w5_1")
-        y1 = [staged([P, 4, half], F32, "y1", 8192 + 6144 * u) for u in range(2)]
+        y1 = [staged([P, half, 4], F32, "y1", 8192 + 6144 * u) for u in range(2)]
         pr_rounded, pr_late = {}, {}
         for u in range(2):
-            for slices in (slice(0, 3), slice(3, 4)):
-                bound(y1[u], 1, slices, halves[u])
+            bound(y1[u][:], 1, halves[u])
             pr_rounded[u] = round_plain(pr_raw[1], halves[u], True, [8192 + 4096, "x1"][u])
 
         flags = {}
@@ -281,14 +284,11 @@ def tile_list_judge_disagreement_audit_kernel(
                 rhs=rhs.bitcast(FP8X4), rhs_scale=rhs_plane, start=start, stop=stop,
             )
 
-        def late_prompt_passes(u):
-            for j, rows in enumerate(blocks):
-                add_pass(u, j, w5_q[1][0][:, rows], w5_q[1][1][:, rows], pr_late[u][0][:], pr_late[u][1][:])
-
         def finish(u, z1):
             cols = halves[u]
             result = kept([P, N // P, half], F32, "result%d" % u)
             for j, rows in enumerate(blocks):
+                add_pass(u, j, w5_q[1][0][:, rows], w5_q[1][1][:, rows], pr_late[u][0][:], pr_late[u][1][:])
                 add_pass(u, j, w4_sb[:, 1, rows], w4_plane[4:P, rows], z1[0][:], z1[1][:], stop=True)
                 nc.scalar.activation(out=result[:, j, :], in_=flags[u, j][:], func=ACT.Abs, bias=bias_sb[:, j : j + 1])
                 nc.sync.dma_start(out=out[rows, cols], in_=result[:, j, :])
@@ -306,5 +306,4 @@ def tile_list_judge_disagreement_audit_kernel(
         for u in range(2):
             z1_rounded = with_gain(1, y1[u], "z1%d_rounded" % u)
             pr_late[u] = quantize(pr_rounded[u], "pr_1%d" % u, half)
-            late_prompt_passes(u)
             finish(u, quantize(z1_rounded, "z1%d" % u, half))

@@ -115,16 +115,18 @@ def tile_list_judge_disagreement_audit_kernel(
             nc.vector.quantize_mx(out=codes[:].bitcast(FP8X4), scales=plane[:], in_=rounded[:])
             return codes, plane
 
-        def round_w2(b, a, scalar_share, slot):
+        def round_w2(b, a, scalar_pairs, slot):
             rounded = staged([P, 4 * W], BF16, "w2_rounded", slot)
             dst = rounded[:].rearrange("p (t m j) -> p m j t", t=4, j=4)
             src = w2_raw[b, a][:].rearrange("p j (m t) -> p m j t", t=4)
-            if scalar_share > 0:
-                part = slice(0, scalar_share)
-                nc.scalar.activation(out=dst[:, part], in_=src[:, part], func=ACT.Copy, scale=-1.0)
-            if scalar_share < P:
-                part = slice(scalar_share, P)
-                nc.vector.tensor_scalar(out=dst[:, part], in0=src[:, part], scalar1=-1.0, scalar2=None, op0=ALU.mult)
+            for pair in range(2):
+                part = slice(2 * pair, 2 * pair + 2)
+                if pair < scalar_pairs:
+                    nc.scalar.activation(out=dst[:, :, :, part], in_=src[:, :, :, part], func=ACT.Copy, scale=-1.0)
+                else:
+                    nc.vector.tensor_scalar(
+                        out=dst[:, :, :, part], in0=src[:, :, :, part], scalar1=-1.0, scalar2=None, op0=ALU.mult
+                    )
             return rounded
 
         def round_plain(raw, cols, on_scalar, slot):
@@ -214,12 +216,12 @@ def tile_list_judge_disagreement_audit_kernel(
         order_w1_scales(0, "w1_plane0")
         gather_words(0)
         sweep(0, 1, 0, start=True)
-        rounded = round_w2(0, 0, 80, "r00")
+        rounded = round_w2(0, 0, 1, "r00")
         order_w1_scales(1, "big0")
         w2_q[0, 0] = quantize(rounded, "w2_00")
         sweep(0, 2, 0)
         gather_words(1)
-        w2_q[0, 1] = quantize(round_w2(0, 1, 64, "r01"), "w2_01")
+        w2_q[0, 1] = quantize(round_w2(0, 1, 1, "r01"), "w2_01")
 
         w5_raw[0] = load_rows(w5, 0, slice(0, N), 0)
         pr_raw[0] = load_rows(prompts, 0, slice(0, M), "big1")

@@ -225,7 +225,7 @@ def tile_list_judge_disagreement_audit_kernel(
 
         w5_raw[0] = load_rows(w5, 0, slice(0, N), 0)
         pr_raw[0] = load_rows(prompts, 0, slice(0, M), "big1")
-        w5_raw[1] = load_rows(w5, 1, slice(0, N), 8192)
+        w5_raw[1] = load_rows(w5, 1, slice(0, N), "big3")
         pr_raw[1] = load_rows(prompts, 1, slice(0, M), "big4")
         gain_sb = kept([P, 2, 4], F32, "gain_sb")
         nc.sync.dma_start(out=gain_sb[:], in_=gain.rearrange("(b p t) -> p b t", b=2, t=4))
@@ -264,17 +264,15 @@ def tile_list_judge_disagreement_audit_kernel(
             close(1, t, last, [0, 4096, "r00", "h13"][t])
             if t >= 2:
                 bound(y0[:, halves[t - 2], :], 0, halves[t - 2])
-        for t in range(3):
+        for t in range(4):
             pick(1, t)
-            if t == 0:
-                pr_q[0] = quantize(pr_rounded, "pr_0")
-        pick(1, 3)
+        pr_q[0] = quantize(pr_rounded, "pr_0", slot="x0")
         w5_q[1] = quantize(round_plain(w5_raw[1], every, True, "w2_11"), "w5_1")
-        y1 = [staged([P, half, 4], F32, "y1", 8192 + 6144 * u) for u in range(2)]
+        y1 = [staged([P, half, 4], F32, "y1", "y1%d" % u) for u in range(2)]
         pr_rounded, pr_late = {}, {}
         for u in range(2):
             bound(y1[u][:], 1, halves[u])
-            pr_rounded[u] = round_plain(pr_raw[1], halves[u], True, [8192 + 4096, "x1"][u])
+            pr_rounded[u] = round_plain(pr_raw[1], halves[u], True, "pr_rounded%d" % u)
 
         flags = {}
 

@@ -50,93 +50,92 @@ def tile_list_judge_disagreement_audit_kernel(
         tab_plane = kept([P, T], U8, "tab_plane")
         w1_plane_raw = kept([P, 2 * H], U8, "w1_plane_raw")
         v_rows = kept([P, S], U8, "v_rows")
-        v_plane = [kept([P, S], U8, "v_plane%d" % a) for a in range(2)]
+        v_plane1 = kept([P, S], U8, "v_plane1")
+        w4_plane = kept([P, N], U8, "w4_plane")
         warm = kept([P, 1], F32, "warm")
 
+        nc.gpsimd.memset(tab_plane[:].bitcast(I32), 0)
         nc.gpsimd.memset(w1_plane_raw[:].bitcast(I32), 0)
-        nc.vector.memset(tab_plane[0:96, :].bitcast(I32), 0)
-        for plane in v_plane:
-            nc.gpsimd.memset(plane[:].bitcast(I32), 0)
+        nc.gpsimd.memset(v_plane1[:].bitcast(I32), 0)
+        nc.gpsimd.memset(w4_plane[:].bitcast(I32), 0)
         nc.vector.memset(warm[:], 0.0)
         nc.scalar.activation(out=warm[:], in_=warm[:], func=ACT.Tanh)
 
-        tab_sb, w1_raw, w1_sb, w1_plane, v_words = {}, {}, {}, {}, {}
-        w2_raw, w2_q, w5_raw, w5_q, pr_raw, pr_q = {}, {}, {}, {}, {}, {}
-        acc, h = {}, {}
-        x = [staged([P, 4, M], F32, "x", "x%d" % b) for b in range(2)]
+        tab_sb, w1_raw, w1_sb, v_words = {}, {}, {}, {}
+        w1_plane = kept([P, 2, 2, W], U8, "w1_plane")
+        w2_raw, w2_rounded, w2_q, w5_raw, w5_q, pr_raw, pr_q = {}, {}, {}, {}, {}, {}, {}
+        acc, h, x, y = {}, {}, {}, {}
+        half = M // 2
+        every = slice(0, M)
+        halves = [slice(0, half), slice(half, M)]
+        blocks = [slice(P * j, P * (j + 1)) for j in range(N // P)]
 
         def load_table(a, slot):
             tab_sb[a] = staged([P, T], I32, "tab_sb", slot)
             nc.sync.dma_start(out=tab_sb[a][:], in_=tab_words[a].rearrange("p t i -> p (t i)").bitcast(I32))
 
-        def load_w1(b):
-            w1_raw[b] = kept([P, 2, W // 2], I32, "w1_raw%d" % b)
+        def load_w1(b, passes):
+            count = passes.stop - passes.start
+            raw = kept([P, count, W // 2], I32, "w1_raw%d%d" % (b, passes.start))
             nc.sync.dma_start(
-                out=w1_raw[b][:],
-                in_=w1_words.bitcast(I32)[:, :, W // 2 * b : W // 2 * (b + 1)].rearrange("a p c -> p a c"),
+                out=raw[:],
+                in_=w1_words.bitcast(I32)[passes, :, W // 2 * b : W // 2 * (b + 1)].rearrange("a p c -> p a c"),
             )
+            return raw
 
         def load_rows(src, a, cols, slot):
-            raw = staged([P, 4, W], F32, "raw", slot)
+            raw = staged([P, 4, cols.stop - cols.start], F32, "raw", slot)
             nc.sync.dma_start(out=raw[:], in_=src[W * a : W * (a + 1), cols].rearrange("(p j) c -> p j c", j=4))
             return raw
 
-        def place_scale_rows(a):
-            for q in range(4):
-                first = 96 + 16 * a + 4 * q
-                nc.sync.dma_start(
-                    out=v_plane[a][32 * q : 32 * q + 4, :].bitcast(I32), in_=v_rows[first : first + 4, :].bitcast(I32)
-                )
-
-        def order_w1_words(b, slot):
-            w1_sb[b] = staged([P, 2, 2 * W], U8, "w1_sb", slot)
+        def order_w1_words(b, passes, raw):
             nc.vector.tensor_copy(
-                out=w1_sb[b][:].bitcast(U16).rearrange("p a (t m) -> p a t m", t=4),
-                in_=w1_raw[b][:].bitcast(U16).rearrange("p a (m t) -> p a t m", t=4),
+                out=w1_sb[b][:, passes, :].bitcast(U16).rearrange("p a (t m) -> p a t m", t=4),
+                in_=raw[:].bitcast(U16).rearrange("p a (m t) -> p a t m", t=4),
             )
 
-        def order_w1_scales(b, slot):
-            w1_plane[b] = staged([P, 2, W], U8, "w1_plane", slot)
+        def order_w1_scales(groups):
             nc.vector.tensor_copy(
-                out=w1_plane[b][:].rearrange("p a (t m) -> p a t m", t=4),
-                in_=w1_plane_raw[:].rearrange("p (a b m t) -> p b a t m", a=2, b=2, t=4)[:, b],
+                out=w1_plane[:].rearrange("p a b (t m) -> p (a b) t m", t=4)[:, groups],
+                in_=w1_plane_raw[:].rearrange("p (g m t) -> p g t m", g=4, t=4)[:, groups],
             )
 
-        def gather_words(a):
-            for c in range(2):
-                v_words[a, c] = kept([P, W], U32, "v_words%d%d" % (a, c))
-                nc.vector.tensor_copy(
-                    v_words[a, c][:], tab_sb[a][:].bitcast(U32).indirect(idx[:, 32 * c : 32 * (c + 1)])
-                )
+        def gather_words(a, c, slot=None):
+            name = "v_words%d%d" % (a, c)
+            v_words[a, c] = staged([P, W], U32, name, slot or name)
+            nc.vector.tensor_copy(v_words[a, c][:], tab_sb[a][:].bitcast(U32).indirect(idx[:, 32 * c : 32 * (c + 1)]))
 
-        def quantize(rounded, name, width=W, slot=None):
-            codes = staged([P, width], U32, name, slot or name)
+        def quantize(rounded, name, slot=None):
+            width = rounded.shape[1] // 4
+            codes = staged([P, width], U32, name, name if slot is None else slot)
             plane = kept([P, width], U8, name + "_plane")
-            nc.vector.quantize_mx(out=codes[:].bitcast(FP8X4), scales=plane[:], in_=rounded[:])
+            nc.vector.quantize_mx(out=codes[:].bitcast(FP8X4), scales=plane[:], in_=rounded)
             return codes, plane
 
-        def round_w2(b, a, scalar_pairs, slot):
-            rounded = staged([P, 4 * W], BF16, "w2_rounded", slot)
-            dst = rounded[:].rearrange("p (t m j) -> p m j t", t=4, j=4)
-            src = w2_raw[b, a][:].rearrange("p j (m t) -> p m j t", t=4)
-            for pair in range(2):
+        def round_w2(rounded, raw, first, pairs, on_scalar):
+            width = raw[:].shape[2] // 4
+            dst = rounded[:].rearrange("p (t m j) -> p m j t", t=4, j=4)[:, first : first + width]
+            src = raw[:].rearrange("p j (m t) -> p m j t", t=4)
+            for pair in pairs:
                 part = slice(2 * pair, 2 * pair + 2)
-                if pair < scalar_pairs:
+                if on_scalar:
                     nc.scalar.activation(out=dst[:, :, :, part], in_=src[:, :, :, part], func=ACT.Copy, scale=-1.0)
                 else:
                     nc.vector.tensor_scalar(
                         out=dst[:, :, :, part], in0=src[:, :, :, part], scalar1=-1.0, scalar2=None, op0=ALU.mult
                     )
-            return rounded
 
-        def round_plain(raw, cols, on_scalar, slot):
-            rounded = staged([P, 4 * (cols.stop - cols.start)], BF16, "rounded", slot)
-            dst = rounded[:].rearrange("p (c i j) -> p c j i", i=4, j=4)
-            src = raw[:, :, cols].rearrange("p j (c i) -> p c j i", i=4)
+        def round_into(rounded, raw, on_scalar):
+            dst = rounded.rearrange("p (c i j) -> p c j i", i=4, j=4)
+            src = raw.rearrange("p j (c i) -> p c j i", i=4)
             if on_scalar:
                 nc.scalar.activation(out=dst, in_=src, func=ACT.Copy)
             else:
                 nc.vector.tensor_copy(out=dst, in_=src)
+
+        def round_plain(raw, cols, on_scalar, slot):
+            rounded = staged([P, 4 * (cols.stop - cols.start)], BF16, "rounded", slot)
+            round_into(rounded[:], raw[:, :, cols], on_scalar)
             return rounded
 
         def score_pass(b, t, c, weight, a, start=False, stop=False):
@@ -145,134 +144,161 @@ def tile_list_judge_disagreement_audit_kernel(
             cols = slice(W * c, W * (c + 1))
             if weight == 1:
                 lhs = w1_sb[b][:, a, 2 * P * t : 2 * P * (t + 1)].bitcast(FP4X4)
-                lhs_plane = w1_plane[b][:, a, P * t : P * (t + 1)]
+                lhs_plane = w1_plane[:, a, b, P * t : P * (t + 1)]
+                rhs_plane = [v_rows, v_plane1][a][:, cols]
             else:
-                lhs = w2_q[b, a][0][:, P * t : P * (t + 1)].bitcast(FP8X4)
-                lhs_plane = w2_q[b, a][1][:, P * t : P * (t + 1)]
+                codes, plane, first = w2_q[b, a, t]
+                lhs = codes[:, first : first + P].bitcast(FP8X4)
+                lhs_plane = plane[:, first : first + P]
+                rhs_plane = v_rows[4 * a : P, cols]
             nc.tensor.matmul_mx(
                 out=acc[b, t, c][:], lhsT=lhs, lhsT_scale=lhs_plane,
-                rhs=v_words[a, c][:].bitcast(FP8X4), rhs_scale=v_plane[a][:, cols], start=start, stop=stop,
+                rhs=v_words[a, c][:].bitcast(FP8X4), rhs_scale=rhs_plane, start=start, stop=stop,
             )
 
-        def sweep(b, weight, a, start=False):
-            for c in range(2):
-                for t in range(4):
-                    score_pass(b, t, c, weight, a, start=start)
+        def quantize_w2(b, a, slices, slot=None):
+            part = w2_rounded[b, a][:, W * slices[0] : W * (slices[-1] + 1)]
+            codes, plane = quantize(part, "w2_%d%d%d" % (b, a, slices[0]), slot)
+            for t in slices:
+                w2_q[b, a, t] = (codes, plane, P * (t - slices[0]))
 
-        def close(b, t, a, slot):
+        def sweep(b, a, c, start=False):
+            for t in range(4):
+                score_pass(b, t, c, 1, a, start=start)
+
+        def close(b, t, slot):
             h[b, t] = staged([P, S], F32, "h", slot)
             for c in range(2):
-                score_pass(b, t, c, 2, a, stop=True)
+                last = 1 if t == 0 else 0
+                score_pass(b, t, c, 2, 1 - last)
+                score_pass(b, t, c, 2, last, stop=True)
                 nc.scalar.copy(out=h[b, t][:, W * c : W * (c + 1)], in_=acc[b, t, c][:])
 
-        def pick(b, t, parts=1):
-            width = M // parts
-            for u in range(parts):
-                cols = slice(width * u, width * (u + 1))
-                picks = idx2[:, width // 16 * u : width // 16 * (u + 1)]
-                nc.vector.tensor_tensor(x[b][:, t, cols], h[b, t][:].indirect(picks), wgt_sb[:, cols], ALU.mult)
+        def pick(b, t):
+            nc.vector.tensor_tensor(x[b][:, t, :], h[b, t][:].indirect(idx2[:]), wgt_sb[:], ALU.mult)
 
-        def bound(dst, b, cols):
-            nc.scalar.activation(
-                out=dst.rearrange("p (c i) t -> p c t i", i=4),
-                in_=x[b][:, :, cols].rearrange("p t (c i) -> p c t i", i=4),
-                func=ACT.Tanh,
-            )
+        def bound(b, slices, cols):
+            nc.scalar.activation(out=y[b][:, slices, cols], in_=x[b][:, slices, cols], func=ACT.Tanh)
 
-        def with_gain(b, src, slot):
-            width = src.shape[1]
-            rounded = staged([P, 4 * width], BF16, "z_rounded", slot)
+        def with_gain(b, cols, rounded):
+            width = cols.stop - cols.start
             nc.vector.tensor_tensor(
-                rounded[:].rearrange("p (m t) -> p m t", t=4),
-                src[:],
-                gain_sb[:, b, :].unsqueeze(1).broadcast_to([P, width, 4]),
+                rounded.rearrange("p (c i t) -> p c t i", i=4, t=4),
+                y[b][:, :, cols].rearrange("p t (c i) -> p c t i", i=4),
+                gain_sb[:, b, :].unsqueeze(1).unsqueeze(3).broadcast_to([P, width // 4, 4, 4]),
                 ALU.mult,
             )
-            return rounded
 
-        nc.sync.dma_start(out=tab_plane[96:P, :].bitcast(I32), in_=tab_scales.rearrange("a q t -> (a q) t").bitcast(I32))
+        first_pass, second_pass, both = slice(0, 1), slice(1, 2), slice(0, 2)
         nc.sync.dma_start(idx[:], offs)
-        load_w1(0)
+        w1_raw[0, 0] = load_w1(0, first_pass)
+        load_scale_rows(tab_plane, 0, tab_scales)
+        load_table(0, "big0")
         for q in range(4):
             nc.sync.dma_start(
                 out=w1_plane_raw[32 * q : 32 * q + 4, :].bitcast(I32).rearrange("r (a c) -> r a c", a=2),
                 in_=w1_scales[:, 4 * q : 4 * q + 4, :].bitcast(I32).rearrange("a r c -> r a c"),
             )
-        load_table(0, "big0")
-        w2_raw[0, 0] = load_rows(w2, 0, slice(0, W), "big1")
+        w1_raw[0, 1] = load_w1(0, second_pass)
+        load_table(1, "big1")
+        w2_raw[0, 0, 0] = load_rows(w2, 0, halves[0], "w2a")
+        for b in range(2):
+            w1_sb[b] = kept([P, 2, 2 * W], U8, "w1_sb%d" % b)
+            x[b] = kept([P, 4, M], F32, "x%d" % b)
+        order_w1_words(0, first_pass, w1_raw[0, 0])
         nc.vector.tensor_copy(v_rows[:], tab_plane[:].indirect(idx[:]))
-        place_scale_rows(0)
-        load_table(1, "big2")
-        w2_raw[0, 1] = load_rows(w2, 1, slice(0, W), "big3")
-        place_scale_rows(1)
-        w2_raw[1, 0] = load_rows(w2, 0, slice(W, 2 * W), "big4")
-        load_w1(1)
-        w2_raw[1, 1] = load_rows(w2, 1, slice(W, 2 * W), "big5")
+        for q in range(4):
+            nc.sync.dma_start(
+                out=v_plane1[32 * q : 32 * q + 4, :].bitcast(I32), in_=v_rows[32 * q + 4 : 32 * q + 8, :].bitcast(I32)
+            )
+        w2_raw[0, 0, 1] = load_rows(w2, 0, halves[1], "w2b")
+        w2_raw[0, 1, 0] = load_rows(w2, 1, halves[0], "w2c")
+        w2_raw[0, 1, 1] = load_rows(w2, 1, halves[1], "w2d")
+        w2_raw[1, 0, 0] = load_rows(w2, 0, slice(W, W + half), "w2e")
+        w2_raw[1, 0, 1] = load_rows(w2, 0, slice(W + half, 2 * W), "w2f")
+        w1_raw[1] = load_w1(1, both)
         wgt_sb = kept([P, M], F32, "wgt_sb")
         nc.sync.dma_start(out=wgt_sb[:], in_=wgt)
         nc.sync.dma_start(idx2[:], offs2)
-
-        order_w1_words(0, "w1_sb0")
-        order_w1_scales(0, "w1_plane0")
-        gather_words(0)
-        sweep(0, 1, 0, start=True)
-        rounded = round_w2(0, 0, 1, "r00")
-        order_w1_scales(1, "big0")
-        w2_q[0, 0] = quantize(rounded, "w2_00")
-        sweep(0, 2, 0)
-        gather_words(1)
-        w2_q[0, 1] = quantize(round_w2(0, 1, 1, "r01"), "w2_01")
-
-        w5_raw[0] = load_rows(w5, 0, slice(0, N), 0)
-        pr_raw[0] = load_rows(prompts, 0, slice(0, M), "big1")
-        w5_raw[1] = load_rows(w5, 1, slice(0, N), "big3")
-        pr_raw[1] = load_rows(prompts, 1, slice(0, M), "big4")
+        w2_raw[1, 1] = load_rows(w2, 1, slice(W, 2 * W), "big3")
+        w5_raw[0] = [load_rows(w5, 0, halves[u], "w5_raw0%d" % u) for u in range(2)]
         gain_sb = kept([P, 2, 4], F32, "gain_sb")
         nc.sync.dma_start(out=gain_sb[:], in_=gain.rearrange("(b p t) -> p b t", b=2, t=4))
+        w5_raw[1] = load_rows(w5, 1, every, 0)
+        pr_raw[0] = load_rows(prompts, 0, every, "big1")
+        pr_raw[1] = load_rows(prompts, 1, every, "big5")
         w4_sb = kept([P, 2, N], I32, "w4_sb")
         nc.sync.dma_start(out=w4_sb[:], in_=w4_words.rearrange("a p c i -> p a (c i)").bitcast(I32))
-        w4_plane = kept([P, N], U8, "w4_plane")
-        nc.gpsimd.memset(w4_plane[:].bitcast(I32), 0)
         load_scale_rows(w4_plane, 0, w4_scales)
         bias_sb = kept([P, N // P], F32, "bias_sb")
         with nc.allow_non_contiguous_dma(reason="one bias value for each output row"):
             nc.sync.dma_start(out=bias_sb[:], in_=bias.rearrange("(j p) -> p j", p=P))
 
+        gather_words(0, 0)
+        order_w1_scales(slice(0, 1))
+        sweep(0, 0, 0, start=True)
+        order_w1_scales(slice(2, 3))
+        order_w1_scales(slice(1, 4, 2))
+        order_w1_words(0, second_pass, w1_raw[0, 1])
+        gather_words(0, 1, "w1_plane_raw")
+        sweep(0, 0, 1, start=True)
+        gather_words(1, 0)
+        sweep(0, 1, 0)
+        gather_words(1, 1)
+        sweep(0, 1, 1)
+        for a in range(2):
+            w2_rounded[0, a] = kept([P, 4 * W], BF16, "r0%d" % a)
+        round_w2(w2_rounded[0, 0], w2_raw[0, 0, 0], 0, range(2), True)
+        round_w2(w2_rounded[0, 0], w2_raw[0, 0, 1], P // 2, range(2), True)
+        quantize_w2(0, 0, range(4))
+        round_w2(w2_rounded[0, 1], w2_raw[0, 1, 0], 0, range(2), True)
+        round_w2(w2_rounded[0, 1], w2_raw[0, 1, 1], P // 2, [0], False)
+        round_w2(w2_rounded[0, 1], w2_raw[0, 1, 1], P // 2, [1], True)
+        quantize_w2(0, 1, [0, 1])
+        quantize_w2(0, 1, [2, 3])
+        w2_rounded[1, 0] = staged([P, 4 * W], BF16, "r10", "r10")
+        round_w2(w2_rounded[1, 0], w2_raw[1, 0, 0], 0, range(2), False)
+        round_w2(w2_rounded[1, 0], w2_raw[1, 0, 1], P // 2, range(2), False)
+        order_w1_words(1, both, w1_raw[1])
+        quantize_w2(1, 0, range(4))
         for t in range(4):
+            close(0, t, "h0%d" % t)
+        for a in range(2):
             for c in range(2):
-                score_pass(0, t, c, 1, 1)
-            close(0, t, 1, "h0%d" % t)
-        rounded = round_w2(1, 0, 0, "r10")
-        order_w1_words(1, "w1_sb1")
-        w2_q[1, 0] = quantize(rounded, "w2_10")
-        w2_q[1, 1] = quantize(round_w2(1, 1, 0, "r11"), "w2_11")
+                sweep(1, a, c, start=(a == 0))
         for t in range(4):
             pick(0, t)
-        half = M // 2
-        every = slice(0, M)
-        halves = [slice(0, half), slice(half, M)]
-        blocks = [slice(P * j, P * (j + 1)) for j in range(N // P)]
-        w5_q[0] = quantize(round_plain(w5_raw[0], every, True, "r00"), "w5_0")
-        pr_rounded = round_plain(pr_raw[0], every, False, "r10")
-        y0 = staged([P, M, 4], F32, "y0", "big1")
+        y[0] = kept([P, 4, M], F32, "y0")
+        for t in range(2):
+            bound(0, slice(t, t + 1), every)
+        w2_rounded[1, 1] = staged([P, 4 * W], BF16, "r11", "w2_000")
+        round_w2(w2_rounded[1, 1], w2_raw[1, 1], 0, [0], False)
+        round_w2(w2_rounded[1, 1], w2_raw[1, 1], 0, [1], True)
+        quantize_w2(1, 1, [2, 3])
+        quantize_w2(1, 1, [0, 1])
+        y[1] = staged([P, 4, M], F32, "y1", "big3")
+        for t in range(2, 4):
+            bound(0, slice(t, t + 1), every)
+        w5_rounded = staged([P, 4 * N], BF16, "rounded", "r00")
+        for u in range(2):
+            round_into(w5_rounded[:, 4 * half * u : 4 * half * (u + 1)], w5_raw[0][u][:], u == 0)
+        z0_rounded = kept([P, 4 * M], BF16, "z0_rounded")
+        for cols in halves:
+            with_gain(0, cols, z0_rounded[:, 4 * cols.start : 4 * cols.stop])
+        w5_q[0] = quantize(w5_rounded[:], "w5_0")
         for t in range(4):
-            last = 1 if t < 2 else 0
-            for c in range(2):
-                score_pass(1, t, c, 2, 1 - last, start=True)
-                score_pass(1, t, c, 1, 0)
-                score_pass(1, t, c, 1, 1)
-            close(1, t, last, [0, 4096, "r00", "h13"][t])
-            if t >= 2:
-                bound(y0[:, halves[t - 2], :], 0, halves[t - 2])
+            close(1, t, "h1%d" % t)
         for t in range(4):
             pick(1, t)
-        pr_q[0] = quantize(pr_rounded, "pr_0", slot="x0")
-        w5_q[1] = quantize(round_plain(w5_raw[1], every, True, "w2_11"), "w5_1")
-        y1 = [staged([P, half, 4], F32, "y1", "y1%d" % u) for u in range(2)]
-        pr_rounded, pr_late = {}, {}
+        w5_rounded = round_plain(w5_raw[1], every, True, "w2_100")
+        z0 = quantize(z0_rounded[:], "z0", 0)
+        w5_q[1] = quantize(w5_rounded[:], "w5_1")
+        pr_rounded = {}
+        pr_rounded[0, 0] = round_plain(pr_raw[0], halves[0], True, "v_words00")
+        pr_rounded[1, 0] = round_plain(pr_raw[1], halves[0], False, 2048)
         for u in range(2):
-            bound(y1[u][:], 1, halves[u])
-            pr_rounded[u] = round_plain(pr_raw[1], halves[u], True, "pr_rounded%d" % u)
+            bound(1, slice(0, 4), halves[u])
+            pr_rounded[u, 1] = round_plain(pr_raw[u], halves[1], True, "pr_rounded%d1" % u)
 
         flags = {}
 
@@ -284,26 +310,20 @@ def tile_list_judge_disagreement_audit_kernel(
                 rhs=rhs.bitcast(FP8X4), rhs_scale=rhs_plane, start=start, stop=stop,
             )
 
-        def finish(u, z1):
-            cols = halves[u]
+        for u in range(2):
+            for j, rows in enumerate(blocks):
+                add_pass(u, j, w4_sb[:, 0, rows], w4_plane[:, rows], z0[0][:, halves[u]], z0[1][:, halves[u]], start=True)
+        for u, cols in enumerate(halves):
+            pr_q[0, u] = quantize(pr_rounded[0, u][:], "pr_0%d" % u)
+            z1_rounded = kept([P, 4 * half], BF16, "z1%d_rounded" % u)
+            with_gain(1, cols, z1_rounded[:])
+            pr_q[1, u] = quantize(pr_rounded[1, u][:], "pr_1%d" % u)
+            z1 = quantize(z1_rounded[:], "z1%d" % u)
+            for j, rows in enumerate(blocks):
+                add_pass(u, j, w5_q[0][0][:, rows], w5_q[0][1][:, rows], pr_q[0, u][0][:], pr_q[0, u][1][:])
             result = kept([P, N // P, half], F32, "result%d" % u)
             for j, rows in enumerate(blocks):
-                add_pass(u, j, w5_q[1][0][:, rows], w5_q[1][1][:, rows], pr_late[u][0][:], pr_late[u][1][:])
+                add_pass(u, j, w5_q[1][0][:, rows], w5_q[1][1][:, rows], pr_q[1, u][0][:], pr_q[1, u][1][:])
                 add_pass(u, j, w4_sb[:, 1, rows], w4_plane[4:P, rows], z1[0][:], z1[1][:], stop=True)
                 nc.scalar.activation(out=result[:, j, :], in_=flags[u, j][:], func=ACT.Abs, bias=bias_sb[:, j : j + 1])
                 nc.sync.dma_start(out=out[rows, cols], in_=result[:, j, :])
-
-        def z0_passes(u):
-            for j, rows in enumerate(blocks):
-                add_pass(u, j, w4_sb[:, 0, rows], w4_plane[:, rows], z0[0][:, halves[u]], z0[1][:, halves[u]])
-
-        for u, cols in enumerate(halves):
-            for j, rows in enumerate(blocks):
-                add_pass(u, j, w5_q[0][0][:, rows], w5_q[0][1][:, rows], pr_q[0][0][:, cols], pr_q[0][1][:, cols], start=True)
-        z0 = quantize(with_gain(0, y0, "z0_rounded"), "z0")
-        for u in range(2):
-            z0_passes(u)
-        for u in range(2):
-            z1_rounded = with_gain(1, y1[u], "z1%d_rounded" % u)
-            pr_late[u] = quantize(pr_rounded[u], "pr_1%d" % u, half)
-            finish(u, quantize(z1_rounded, "z1%d" % u, half))

@@ -50,19 +50,20 @@ def tile_list_judge_disagreement_audit_kernel(
         tab_plane = kept([P, T], U8, "tab_plane")
         w1_plane_raw = kept([P, 2 * H], U8, "w1_plane_raw")
         v_rows = kept([P, S], U8, "v_rows")
-        v_plane1 = kept([P, S], U8, "v_plane1")
+        v_plane = [kept([P, S], U8, "v_plane%d" % a) for a in range(2)]
         w4_plane = kept([P, N], U8, "w4_plane")
         warm = kept([P, 1], F32, "warm")
 
-        nc.gpsimd.memset(tab_plane[:].bitcast(I32), 0)
         nc.gpsimd.memset(w1_plane_raw[:].bitcast(I32), 0)
-        nc.gpsimd.memset(v_plane1[:].bitcast(I32), 0)
+        nc.vector.memset(tab_plane[0:96, :].bitcast(I32), 0)
+        for plane in v_plane:
+            nc.gpsimd.memset(plane[:].bitcast(I32), 0)
         nc.gpsimd.memset(w4_plane[:].bitcast(I32), 0)
         nc.vector.memset(warm[:], 0.0)
         nc.scalar.activation(out=warm[:], in_=warm[:], func=ACT.Tanh)
 
         tab_sb, w1_raw, w1_sb, v_words = {}, {}, {}, {}
-        w1_plane = kept([P, 2, 2, W], U8, "w1_plane")
+        w1_plane = {}
         w2_raw, w2_rounded, w2_q, w5_raw, w5_q, pr_raw, pr_q = {}, {}, {}, {}, {}, {}, {}
         acc, h, x, y = {}, {}, {}, {}
         half = M // 2
@@ -70,9 +71,15 @@ def tile_list_judge_disagreement_audit_kernel(
         halves = [slice(0, half), slice(half, M)]
         blocks = [slice(P * j, P * (j + 1)) for j in range(N // P)]
 
-        def load_table(a, slot):
-            tab_sb[a] = staged([P, T], I32, "tab_sb", slot)
-            nc.sync.dma_start(out=tab_sb[a][:], in_=tab_words[a].rearrange("p t i -> p (t i)").bitcast(I32))
+        def load_table(a, cols):
+            nc.sync.dma_start(out=tab_sb[a][:, cols], in_=tab_words[a].rearrange("p t i -> p (t i)").bitcast(I32)[:, cols])
+
+        def place_scale_rows(a):
+            for q in range(4):
+                first = 96 + 16 * a + 4 * q
+                nc.sync.dma_start(
+                    out=v_plane[a][32 * q : 32 * q + 4, :].bitcast(I32), in_=v_rows[first : first + 4, :].bitcast(I32)
+                )
 
         def load_w1(b, passes):
             count = passes.stop - passes.start
@@ -94,11 +101,15 @@ def tile_list_judge_disagreement_audit_kernel(
                 in_=raw[:].bitcast(U16).rearrange("p a (m t) -> p a t m", t=4),
             )
 
-        def order_w1_scales(groups):
+        def order_w1_scales(groups, slot):
+            count = len(range(4)[groups])
+            planes = staged([P, count, W], U8, "w1_plane", slot)
             nc.vector.tensor_copy(
-                out=w1_plane[:].rearrange("p a b (t m) -> p (a b) t m", t=4)[:, groups],
+                out=planes[:].rearrange("p g (t m) -> p g t m", t=4),
                 in_=w1_plane_raw[:].rearrange("p (g m t) -> p g t m", g=4, t=4)[:, groups],
             )
+            for i, g in enumerate(range(4)[groups]):
+                w1_plane[divmod(g, 2)] = planes[:, i, :]
 
         def gather_words(a, c, slot=None):
             name = "v_words%d%d" % (a, c)
@@ -144,16 +155,14 @@ def tile_list_judge_disagreement_audit_kernel(
             cols = slice(W * c, W * (c + 1))
             if weight == 1:
                 lhs = w1_sb[b][:, a, 2 * P * t : 2 * P * (t + 1)].bitcast(FP4X4)
-                lhs_plane = w1_plane[:, a, b, P * t : P * (t + 1)]
-                rhs_plane = [v_rows, v_plane1][a][:, cols]
+                lhs_plane = w1_plane[a, b][:, P * t : P * (t + 1)]
             else:
                 codes, plane, first = w2_q[b, a, t]
                 lhs = codes[:, first : first + P].bitcast(FP8X4)
                 lhs_plane = plane[:, first : first + P]
-                rhs_plane = v_rows[4 * a : P, cols]
             nc.tensor.matmul_mx(
                 out=acc[b, t, c][:], lhsT=lhs, lhsT_scale=lhs_plane,
-                rhs=v_words[a, c][:].bitcast(FP8X4), rhs_scale=rhs_plane, start=start, stop=stop,
+                rhs=v_words[a, c][:].bitcast(FP8X4), rhs_scale=v_plane[a][:, cols], start=start, stop=stop,
             )
 
         def quantize_w2(b, a, slices, slot=None):
@@ -169,10 +178,13 @@ def tile_list_judge_disagreement_audit_kernel(
         def close(b, t, slot):
             h[b, t] = staged([P, S], F32, "h", slot)
             for c in range(2):
-                last = 1 if t == 0 else 0
+                last = 1 if t < 2 - b else 0
                 score_pass(b, t, c, 2, 1 - last)
                 score_pass(b, t, c, 2, last, stop=True)
-                nc.scalar.copy(out=h[b, t][:, W * c : W * (c + 1)], in_=acc[b, t, c][:])
+                if (b, t, c) == (0, 0, 1):
+                    nc.vector.tensor_copy(out=h[b, t][:, W * c : W * (c + 1)], in_=acc[b, t, c][:])
+                else:
+                    nc.scalar.copy(out=h[b, t][:, W * c : W * (c + 1)], in_=acc[b, t, c][:])
 
         def pick(b, t):
             nc.vector.tensor_tensor(x[b][:, t, :], h[b, t][:].indirect(idx2[:]), wgt_sb[:], ALU.mult)
@@ -190,41 +202,38 @@ def tile_list_judge_disagreement_audit_kernel(
             )
 
         first_pass, second_pass, both = slice(0, 1), slice(1, 2), slice(0, 2)
+        nc.sync.dma_start(out=tab_plane[96:P, :].bitcast(I32), in_=tab_scales.rearrange("a q t -> (a q) t").bitcast(I32))
         nc.sync.dma_start(idx[:], offs)
         w1_raw[0, 0] = load_w1(0, first_pass)
-        load_scale_rows(tab_plane, 0, tab_scales)
-        load_table(0, "big0")
         for q in range(4):
             nc.sync.dma_start(
                 out=w1_plane_raw[32 * q : 32 * q + 4, :].bitcast(I32).rearrange("r (a c) -> r a c", a=2),
                 in_=w1_scales[:, 4 * q : 4 * q + 4, :].bitcast(I32).rearrange("a r c -> r a c"),
             )
+        for a in range(2):
+            tab_sb[a] = staged([P, T], I32, "tab_sb", [0, "big1"][a])
+        load_table(0, slice(0, T))
         w1_raw[0, 1] = load_w1(0, second_pass)
-        load_table(1, "big1")
-        w2_raw[0, 0, 0] = load_rows(w2, 0, halves[0], "w2a")
+        load_table(1, slice(0, 1280))
         for b in range(2):
             w1_sb[b] = kept([P, 2, 2 * W], U8, "w1_sb%d" % b)
             x[b] = kept([P, 4, M], F32, "x%d" % b)
-        order_w1_words(0, first_pass, w1_raw[0, 0])
         nc.vector.tensor_copy(v_rows[:], tab_plane[:].indirect(idx[:]))
-        for q in range(4):
-            nc.sync.dma_start(
-                out=v_plane1[32 * q : 32 * q + 4, :].bitcast(I32), in_=v_rows[32 * q + 4 : 32 * q + 8, :].bitcast(I32)
-            )
-        w2_raw[0, 0, 1] = load_rows(w2, 0, halves[1], "w2b")
-        w2_raw[0, 1, 0] = load_rows(w2, 1, halves[0], "w2c")
-        w2_raw[0, 1, 1] = load_rows(w2, 1, halves[1], "w2d")
-        w2_raw[1, 0, 0] = load_rows(w2, 0, slice(W, W + half), "w2e")
-        w2_raw[1, 0, 1] = load_rows(w2, 0, slice(W + half, 2 * W), "w2f")
-        w1_raw[1] = load_w1(1, both)
+        place_scale_rows(0)
+        load_table(1, slice(1280, T))
+        w2_raw[0, 0] = load_rows(w2, 0, slice(0, W), "w2a")
+        place_scale_rows(1)
+        w2_raw[0, 1] = load_rows(w2, 1, slice(0, W), "w2b")
         wgt_sb = kept([P, M], F32, "wgt_sb")
         nc.sync.dma_start(out=wgt_sb[:], in_=wgt)
         nc.sync.dma_start(idx2[:], offs2)
+        w1_raw[1] = load_w1(1, both)
+        w2_raw[1, 0] = load_rows(w2, 0, slice(W, 2 * W), "big2")
         w2_raw[1, 1] = load_rows(w2, 1, slice(W, 2 * W), "big3")
-        w5_raw[0] = [load_rows(w5, 0, halves[u], "w5_raw0%d" % u) for u in range(2)]
+        w5_raw[0] = load_rows(w5, 0, every, "w2a")
         gain_sb = kept([P, 2, 4], F32, "gain_sb")
         nc.sync.dma_start(out=gain_sb[:], in_=gain.rearrange("(b p t) -> p b t", b=2, t=4))
-        w5_raw[1] = load_rows(w5, 1, every, 0)
+        w5_raw[1] = load_rows(w5, 1, every, 8192)
         pr_raw[0] = load_rows(prompts, 0, every, "big1")
         pr_raw[1] = load_rows(prompts, 1, every, "big5")
         w4_sb = kept([P, 2, N], I32, "w4_sb")
@@ -234,33 +243,28 @@ def tile_list_judge_disagreement_audit_kernel(
         with nc.allow_non_contiguous_dma(reason="one bias value for each output row"):
             nc.sync.dma_start(out=bias_sb[:], in_=bias.rearrange("(j p) -> p j", p=P))
 
+        order_w1_words(0, first_pass, w1_raw[0, 0])
+        order_w1_scales(slice(0, 1), "w1_plane00")
         gather_words(0, 0)
-        order_w1_scales(slice(0, 1))
         sweep(0, 0, 0, start=True)
-        order_w1_scales(slice(2, 3))
-        order_w1_scales(slice(1, 4, 2))
-        order_w1_words(0, second_pass, w1_raw[0, 1])
-        gather_words(0, 1, "w1_plane_raw")
+        gather_words(0, 1)
         sweep(0, 0, 1, start=True)
+        order_w1_words(0, second_pass, w1_raw[0, 1])
+        order_w1_scales(slice(2, 3), 0)
         gather_words(1, 0)
         sweep(0, 1, 0)
         gather_words(1, 1)
         sweep(0, 1, 1)
+        order_w1_scales(slice(1, 4, 2), 1024)
         for a in range(2):
             w2_rounded[0, a] = kept([P, 4 * W], BF16, "r0%d" % a)
-        round_w2(w2_rounded[0, 0], w2_raw[0, 0, 0], 0, range(2), True)
-        round_w2(w2_rounded[0, 0], w2_raw[0, 0, 1], P // 2, range(2), True)
-        quantize_w2(0, 0, range(4))
-        round_w2(w2_rounded[0, 1], w2_raw[0, 1, 0], 0, range(2), True)
-        round_w2(w2_rounded[0, 1], w2_raw[0, 1, 1], P // 2, [0], False)
-        round_w2(w2_rounded[0, 1], w2_raw[0, 1, 1], P // 2, [1], True)
+            round_w2(w2_rounded[0, a], w2_raw[0, a], 0, [0], False)
+            round_w2(w2_rounded[0, a], w2_raw[0, a], 0, [1], True)
+            if a == 0:
+                quantize_w2(0, 0, range(4))
         quantize_w2(0, 1, [0, 1])
         quantize_w2(0, 1, [2, 3])
-        w2_rounded[1, 0] = staged([P, 4 * W], BF16, "r10", "r10")
-        round_w2(w2_rounded[1, 0], w2_raw[1, 0, 0], 0, range(2), False)
-        round_w2(w2_rounded[1, 0], w2_raw[1, 0, 1], P // 2, range(2), False)
         order_w1_words(1, both, w1_raw[1])
-        quantize_w2(1, 0, range(4))
         for t in range(4):
             close(0, t, "h0%d" % t)
         for a in range(2):
@@ -268,20 +272,20 @@ def tile_list_judge_disagreement_audit_kernel(
                 sweep(1, a, c, start=(a == 0))
         for t in range(4):
             pick(0, t)
-        y[0] = kept([P, 4, M], F32, "y0")
-        for t in range(2):
-            bound(0, slice(t, t + 1), every)
-        w2_rounded[1, 1] = staged([P, 4 * W], BF16, "r11", "w2_000")
-        round_w2(w2_rounded[1, 1], w2_raw[1, 1], 0, [0], False)
-        round_w2(w2_rounded[1, 1], w2_raw[1, 1], 0, [1], True)
-        quantize_w2(1, 1, [2, 3])
+        w2_rounded[1, 0] = staged([P, 4 * W], BF16, "r10", "w2_000")
+        round_w2(w2_rounded[1, 0], w2_raw[1, 0], 0, range(2), True)
+        w2_rounded[1, 1] = staged([P, 4 * W], BF16, "r11", "r10")
+        round_w2(w2_rounded[1, 1], w2_raw[1, 1], 0, range(2), False)
+        quantize_w2(1, 0, range(4))
         quantize_w2(1, 1, [0, 1])
+        quantize_w2(1, 1, [2, 3])
+        y[0] = kept([P, 4, M], F32, "y0")
         y[1] = staged([P, 4, M], F32, "y1", "big3")
-        for t in range(2, 4):
-            bound(0, slice(t, t + 1), every)
+        for pair in range(2):
+            bound(0, slice(2 * pair, 2 * pair + 2), every)
         w5_rounded = staged([P, 4 * N], BF16, "rounded", "r00")
         for u in range(2):
-            round_into(w5_rounded[:, 4 * half * u : 4 * half * (u + 1)], w5_raw[0][u][:], u == 0)
+            round_into(w5_rounded[:, 4 * half * u : 4 * half * (u + 1)], w5_raw[0][:, :, halves[u]], u == 0)
         z0_rounded = kept([P, 4 * M], BF16, "z0_rounded")
         for cols in halves:
             with_gain(0, cols, z0_rounded[:, 4 * cols.start : 4 * cols.stop])
@@ -291,11 +295,11 @@ def tile_list_judge_disagreement_audit_kernel(
         for t in range(4):
             pick(1, t)
         w5_rounded = round_plain(w5_raw[1], every, True, "w2_100")
-        z0 = quantize(z0_rounded[:], "z0", 0)
+        z0 = quantize(z0_rounded[:], "z0", 8192)
         w5_q[1] = quantize(w5_rounded[:], "w5_1")
         pr_rounded = {}
         pr_rounded[0, 0] = round_plain(pr_raw[0], halves[0], True, "v_words00")
-        pr_rounded[1, 0] = round_plain(pr_raw[1], halves[0], False, 2048)
+        pr_rounded[1, 0] = round_plain(pr_raw[1], halves[0], False, 8192 + 2048)
         for u in range(2):
             bound(1, slice(0, 4), halves[u])
             pr_rounded[u, 1] = round_plain(pr_raw[u], halves[1], True, "pr_rounded%d1" % u)

@@ -123,12 +123,10 @@ def tile_list_judge_disagreement_audit_kernel(
             nc.vector.quantize_mx(out=codes[:].bitcast(FP8X4), scales=plane[:], in_=rounded)
             return codes, plane
 
-        def round_w2(rounded, raw, first, pairs, on_scalar):
-            width = raw[:].shape[2] // 4
-            dst = rounded[:].rearrange("p (t m j) -> p m j t", t=4, j=4)[:, first : first + width]
-            src = raw[:].rearrange("p j (m t) -> p m j t", t=4)
-            for pair in pairs:
-                part = slice(2 * pair, 2 * pair + 2)
+        def round_w2(rounded, raw, span, pairs, on_scalar):
+            dst = rounded[:].rearrange("p (t m j) -> p m j t", t=4, j=4)[:, span]
+            src = raw[:].rearrange("p j (m t) -> p m j t", t=4)[:, span]
+            for part in pairs:
                 if on_scalar:
                     nc.scalar.activation(out=dst[:, :, :, part], in_=src[:, :, :, part], func=ACT.Copy, scale=-1.0)
                 else:
@@ -205,14 +203,14 @@ def tile_list_judge_disagreement_audit_kernel(
         nc.sync.dma_start(out=tab_plane[96:P, :].bitcast(I32), in_=tab_scales.rearrange("a q t -> (a q) t").bitcast(I32))
         nc.sync.dma_start(idx[:], offs)
         w1_raw[0, 0] = load_w1(0, first_pass)
+        for a in range(2):
+            tab_sb[a] = staged([P, T], I32, "tab_sb", [0, "big1"][a])
+        load_table(0, slice(0, T))
         for q in range(4):
             nc.sync.dma_start(
                 out=w1_plane_raw[32 * q : 32 * q + 4, :].bitcast(I32).rearrange("r (a c) -> r a c", a=2),
                 in_=w1_scales[:, 4 * q : 4 * q + 4, :].bitcast(I32).rearrange("a r c -> r a c"),
             )
-        for a in range(2):
-            tab_sb[a] = staged([P, T], I32, "tab_sb", [0, "big1"][a])
-        load_table(0, slice(0, T))
         w1_raw[0, 1] = load_w1(0, second_pass)
         load_table(1, slice(0, 1280))
         for b in range(2):
@@ -244,24 +242,26 @@ def tile_list_judge_disagreement_audit_kernel(
             nc.sync.dma_start(out=bias_sb[:], in_=bias.rearrange("(j p) -> p j", p=P))
 
         order_w1_words(0, first_pass, w1_raw[0, 0])
-        order_w1_scales(slice(0, 1), "w1_plane00")
         gather_words(0, 0)
+        order_w1_scales(slice(0, 1), "w1_plane00")
         sweep(0, 0, 0, start=True)
-        gather_words(0, 1)
-        sweep(0, 0, 1, start=True)
+        order_w1_scales(slice(2, 3), "w1_plane10")
+        order_w1_scales(slice(1, 4, 2), "w1_plane1")
         order_w1_words(0, second_pass, w1_raw[0, 1])
-        order_w1_scales(slice(2, 3), 0)
+        gather_words(0, 1, "w1_plane_raw")
+        sweep(0, 0, 1, start=True)
         gather_words(1, 0)
         sweep(0, 1, 0)
         gather_words(1, 1)
         sweep(0, 1, 1)
-        order_w1_scales(slice(1, 4, 2), 1024)
         for a in range(2):
             w2_rounded[0, a] = kept([P, 4 * W], BF16, "r0%d" % a)
-            round_w2(w2_rounded[0, a], w2_raw[0, a], 0, [0], False)
-            round_w2(w2_rounded[0, a], w2_raw[0, a], 0, [1], True)
-            if a == 0:
-                quantize_w2(0, 0, range(4))
+        round_w2(w2_rounded[0, 0], w2_raw[0, 0], slice(0, P), [slice(0, 2)], False)
+        round_w2(w2_rounded[0, 0], w2_raw[0, 0], slice(0, P), [slice(2, 4)], True)
+        quantize_w2(0, 0, range(4))
+        for pair, share in enumerate([88, 40]):
+            round_w2(w2_rounded[0, 1], w2_raw[0, 1], slice(0, share), [slice(2 * pair, 2 * pair + 2)], False)
+            round_w2(w2_rounded[0, 1], w2_raw[0, 1], slice(share, P), [slice(2 * pair, 2 * pair + 2)], True)
         quantize_w2(0, 1, [0, 1])
         quantize_w2(0, 1, [2, 3])
         order_w1_words(1, both, w1_raw[1])
@@ -273,22 +273,20 @@ def tile_list_judge_disagreement_audit_kernel(
         for t in range(4):
             pick(0, t)
         w2_rounded[1, 0] = staged([P, 4 * W], BF16, "r10", "w2_000")
-        round_w2(w2_rounded[1, 0], w2_raw[1, 0], 0, range(2), True)
+        round_w2(w2_rounded[1, 0], w2_raw[1, 0], slice(0, P), [slice(0, 4)], True)
         w2_rounded[1, 1] = staged([P, 4 * W], BF16, "r11", "r10")
-        round_w2(w2_rounded[1, 1], w2_raw[1, 1], 0, range(2), False)
+        round_w2(w2_rounded[1, 1], w2_raw[1, 1], slice(0, P), [slice(0, 4)], False)
         quantize_w2(1, 0, range(4))
-        quantize_w2(1, 1, [0, 1])
-        quantize_w2(1, 1, [2, 3])
+        quantize_w2(1, 1, range(4))
         y[0] = kept([P, 4, M], F32, "y0")
         y[1] = staged([P, 4, M], F32, "y1", "big3")
         for pair in range(2):
             bound(0, slice(2 * pair, 2 * pair + 2), every)
         w5_rounded = staged([P, 4 * N], BF16, "rounded", "r00")
-        for u in range(2):
-            round_into(w5_rounded[:, 4 * half * u : 4 * half * (u + 1)], w5_raw[0][:, :, halves[u]], u == 0)
+        for cols in [slice(0, 352), slice(352, N)]:
+            round_into(w5_rounded[:, 4 * cols.start : 4 * cols.stop], w5_raw[0][:, :, cols], cols.start == 0)
         z0_rounded = kept([P, 4 * M], BF16, "z0_rounded")
-        for cols in halves:
-            with_gain(0, cols, z0_rounded[:, 4 * cols.start : 4 * cols.stop])
+        with_gain(0, every, z0_rounded[:])
         w5_q[0] = quantize(w5_rounded[:], "w5_0")
         for t in range(4):
             close(1, t, "h1%d" % t)
@@ -299,7 +297,7 @@ def tile_list_judge_disagreement_audit_kernel(
         w5_q[1] = quantize(w5_rounded[:], "w5_1")
         pr_rounded = {}
         pr_rounded[0, 0] = round_plain(pr_raw[0], halves[0], True, "v_words00")
-        pr_rounded[1, 0] = round_plain(pr_raw[1], halves[0], False, 8192 + 2048)
+        pr_rounded[1, 0] = round_plain(pr_raw[1], halves[0], False, "pr_rounded10")
         for u in range(2):
             bound(1, slice(0, 4), halves[u])
             pr_rounded[u, 1] = round_plain(pr_raw[u], halves[1], True, "pr_rounded%d1" % u)

@@ -52,15 +52,12 @@ def tile_list_judge_disagreement_audit_kernel(
         v_rows = kept([P, S], U8, "v_rows")
         v_plane = [kept([P, S], U8, "v_plane%d" % a) for a in range(2)]
         w4_plane = kept([P, N], U8, "w4_plane")
-        warm = kept([P, 1], F32, "warm")
 
         nc.gpsimd.memset(w1_plane_raw[:].bitcast(I32), 0)
         nc.vector.memset(tab_plane[0:96, :].bitcast(I32), 0)
         for plane in v_plane:
             nc.gpsimd.memset(plane[:].bitcast(I32), 0)
         nc.gpsimd.memset(w4_plane[:].bitcast(I32), 0)
-        nc.vector.memset(warm[:], 0.0)
-        nc.scalar.activation(out=warm[:], in_=warm[:], func=ACT.Tanh)
 
         tab_sb, w1_raw, w1_sb, v_words = {}, {}, {}, {}
         w1_plane = {}

@@ -219,10 +219,10 @@ def tile_list_judge_disagreement_audit_kernel(
         w2_raw[0, 0] = load_rows(w2, 0, slice(0, W), "w2a")
         place_scale_rows(1)
         w2_raw[0, 1] = load_rows(w2, 1, slice(0, W), "w2b")
+        w1_raw[1] = load_w1(1, both)
         wgt_sb = kept([P, M], F32, "wgt_sb")
         nc.sync.dma_start(out=wgt_sb[:], in_=wgt)
         nc.sync.dma_start(idx2[:], offs2)
-        w1_raw[1] = load_w1(1, both)
         w2_raw[1, 0] = load_rows(w2, 0, slice(W, 2 * W), "big2")
         w2_raw[1, 1] = load_rows(w2, 1, slice(W, 2 * W), "big3")
         w5_raw[0] = load_rows(w5, 0, every, "w2a")
@@ -259,7 +259,8 @@ def tile_list_judge_disagreement_audit_kernel(
         for pair, share in enumerate([88, 40]):
             round_w2(w2_rounded[0, 1], w2_raw[0, 1], slice(0, share), [slice(2 * pair, 2 * pair + 2)], False)
             round_w2(w2_rounded[0, 1], w2_raw[0, 1], slice(share, P), [slice(2 * pair, 2 * pair + 2)], True)
-        quantize_w2(0, 1, [0, 1])
+        quantize_w2(0, 1, [0])
+        quantize_w2(0, 1, [1])
         quantize_w2(0, 1, [2, 3])
         order_w1_words(1, both, w1_raw[1])
         for t in range(4):

from contextlib import ExitStack

import concourse.mybir as mybir

K, T, S, H, M, N = 1024, 2048, 1024, 1024, 512, 512
FLOPS = 2 * 2 * K * H * S + 2 * (H + K) * N * M

F32 = mybir.dt.float32
BF16 = mybir.dt.bfloat16
I32 = mybir.dt.int32
U32 = mybir.dt.uint32
U16 = mybir.dt.uint16
U8 = mybir.dt.uint8
FP8X4 = mybir.dt.float8_e4m3fn_x4
FP4X4 = mybir.dt.float4_e2m1fn_x4
ACT = mybir.ActivationFunctionType
ALU = mybir.AluOpType

P = 128
W = 512


def tile_list_judge_disagreement_audit_kernel(
    tc, tab_words, tab_scales, offs, offs2, w1_words, w1_scales, w2, wgt, gain,
    w4_words, w4_scales, w5, prompts, bias, out,
):
    nc = tc.nc
    with ExitStack() as ctx:
        keep = ctx.enter_context(tc.tile_pool(name="keep", bufs=1))
        reuse = ctx.enter_context(tc.tile_pool(name="reuse", bufs=1))
        psum = ctx.enter_context(tc.psum_pool(name="psum", bufs=1))

        def kept(shape, dtype, name):
            return keep.tile(shape, dtype, name=name, align_bytes=64)

        def staged(shape, dtype, name, slot):
            if isinstance(slot, int):
                return reuse.tile(shape, dtype, name=name + str(slot), align_bytes=64, offset=slot)
            return keep.tile(shape, dtype, name=name, tag=slot, align_bytes=64)

        def load_scale_rows(plane, first, scales):
            for q in range(4):
                nc.sync.dma_start(
                    out=plane[32 * q + first : 32 * q + first + 8, :].bitcast(I32),
                    in_=scales[:, 4 * q : 4 * q + 4, :].bitcast(I32),
                )

        idx = keep.tile([P, S // 16], U16, name="idx")
        idx2 = keep.tile([P, M // 16], U16, name="idx2")
        tab_plane = kept([P, T], U8, "tab_plane")
        w1_plane_raw = kept([P, 2 * H], U8, "w1_plane_raw")
        v_rows = kept([P, S], U8, "v_rows")
        v_plane = [kept([P, S], U8, "v_plane%d" % a) for a in range(2)]
        w4_plane = kept([P, N], U8, "w4_plane")

        nc.gpsimd.memset(w1_plane_raw[:].bitcast(I32), 0)
        nc.vector.memset(tab_plane[0:96, :].bitcast(I32), 0)
        for plane in v_plane:
            nc.gpsimd.memset(plane[:].bitcast(I32), 0)
        nc.gpsimd.memset(w4_plane[:].bitcast(I32), 0)

        tab_sb, w1_raw, w1_sb, v_words = {}, {}, {}, {}
        w1_plane = {}
        w2_raw, w2_rounded, w2_q, w5_raw, w5_q, pr_raw, pr_q = {}, {}, {}, {}, {}, {}, {}
        acc, h, x, y = {}, {}, {}, {}
        half = M // 2
        every = slice(0, M)
        halves = [slice(0, half), slice(half, M)]
        blocks = [slice(P * j, P * (j + 1)) for j in range(N // P)]

        def load_table(a, cols):
            nc.sync.dma_start(out=tab_sb[a][:, cols], in_=tab_words[a].rearrange("p t i -> p (t i)").bitcast(I32)[:, cols])

        def place_scale_rows(a):
            for q in range(4):
                first = 96 + 16 * a + 4 * q
                nc.sync.dma_start(
                    out=v_plane[a][32 * q : 32 * q + 4, :].bitcast(I32), in_=v_rows[first : first + 4, :].bitcast(I32)
                )

        def load_w1(b, passes):
            count = passes.stop - passes.start
            raw = kept([P, count, W // 2], I32, "w1_raw%d%d" % (b, passes.start))
            nc.sync.dma_start(
                out=raw[:],
                in_=w1_words.bitcast(I32)[passes, :, W // 2 * b : W // 2 * (b + 1)].rearrange("a p c -> p a c"),
            )
            return raw

        def load_rows(src, a, cols, slot):
            raw = staged([P, 4, cols.stop - cols.start], F32, "raw", slot)
            nc.sync.dma_start(out=raw[:], in_=src[W * a : W * (a + 1), cols].rearrange("(p j) c -> p j c", j=4))
            return raw

        def order_w1_words(b, passes, raw):
            nc.vector.tensor_copy(
                out=w1_sb[b][:, passes, :].bitcast(U16).rearrange("p a (t m) -> p a t m", t=4),
                in_=raw[:].bitcast(U16).rearrange("p a (m t) -> p a t m", t=4),
            )

        def order_w1_scales(groups, slot):
            count = len(range(4)[groups])
            planes = staged([P, count, W], U8, "w1_plane", slot)
            nc.vector.tensor_copy(
                out=planes[:].rearrange("p g (t m) -> p g t m", t=4),
                in_=w1_plane_raw[:].rearrange("p (g m t) -> p g t m", g=4, t=4)[:, groups],
            )
            for i, g in enumerate(range(4)[groups]):
                w1_plane[divmod(g, 2)] = planes[:, i, :]

        def gather_words(a, c, slot=None):
            name = "v_words%d%d" % (a, c)
            v_words[a, c] = staged([P, W], U32, name, slot or name)
            nc.vector.tensor_copy(v_words[a, c][:], tab_sb[a][:].bitcast(U32).indirect(idx[:, 32 * c : 32 * (c + 1)]))

        def quantize(rounded, name, slot=None):
            width = rounded.shape[1] // 4
            codes = staged([P, width], U32, name, name if slot is None else slot)
            plane = kept([P, width], U8, name + "_plane")
            nc.vector.quantize_mx(out=codes[:].bitcast(FP8X4), scales=plane[:], in_=rounded)
            return codes, plane

        def round_w2(rounded, raw, span, pairs, on_scalar):
            dst = rounded[:].rearrange("p (t m j) -> p m j t", t=4, j=4)[:, span]
            src = raw[:].rearrange("p j (m t) -> p m j t", t=4)[:, span]
            for part in pairs:
                if on_scalar:
                    nc.scalar.activation(out=dst[:, :, :, part], in_=src[:, :, :, part], func=ACT.Copy, scale=-1.0)
                else:
                    nc.vector.tensor_scalar(
                        out=dst[:, :, :, part], in0=src[:, :, :, part], scalar1=-1.0, scalar2=None, op0=ALU.mult
                    )

        def round_into(rounded, raw, on_scalar):
            dst = rounded.rearrange("p (c i j) -> p c j i", i=4, j=4)
            src = raw.rearrange("p j (c i) -> p c j i", i=4)
            if on_scalar:
                nc.scalar.activation(out=dst, in_=src, func=ACT.Copy)
            else:
                nc.vector.tensor_copy(out=dst, in_=src)

        def round_plain(raw, cols, on_scalar, slot):
            rounded = staged([P, 4 * (cols.stop - cols.start)], BF16, "rounded", slot)
            round_into(rounded[:], raw[:, :, cols], on_scalar)
            return rounded

        def score_pass(b, t, c, weight, a, start=False, stop=False):
            if start:
                acc[b, t, c] = psum.tile([P, W], F32, name="acc", tag="bank%d" % (2 * t + c))
            cols = slice(W * c, W * (c + 1))
            if weight == 1:
                lhs = w1_sb[b][:, a, 2 * P * t : 2 * P * (t + 1)].bitcast(FP4X4)
                lhs_plane = w1_plane[a, b][:, P * t : P * (t + 1)]
            else:
                codes, plane, first = w2_q[b, a, t]
                lhs = codes[:, first : first + P].bitcast(FP8X4)
                lhs_plane = plane[:, first : first + P]
            nc.tensor.matmul_mx(
                out=acc[b, t, c][:], lhsT=lhs, lhsT_scale=lhs_plane,
                rhs=v_words[a, c][:].bitcast(FP8X4), rhs_scale=v_plane[a][:, cols], start=start, stop=stop,
            )

        def quantize_w2(b, a, slices, slot=None):
            part = w2_rounded[b, a][:, W * slices[0] : W * (slices[-1] + 1)]
            codes, plane = quantize(part, "w2_%d%d%d" % (b, a, slices[0]), slot)
            for t in slices:
                w2_q[b, a, t] = (codes, plane, P * (t - slices[0]))

        def sweep(b, a, c, start=False):
            for t in range(4):
                score_pass(b, t, c, 1, a, start=start)

        def close(b, t, slot):
            h[b, t] = staged([P, S], F32, "h", slot)
            for c in range(2):
                last = 1 if t < 2 - b else 0
                score_pass(b, t, c, 2, 1 - last)
                score_pass(b, t, c, 2, last, stop=True)
                if (b, t, c) == (0, 0, 1):
                    nc.vector.tensor_copy(out=h[b, t][:, W * c : W * (c + 1)], in_=acc[b, t, c][:])
                else:
                    nc.scalar.copy(out=h[b, t][:, W * c : W * (c + 1)], in_=acc[b, t, c][:])

        def pick(b, t):
            nc.vector.tensor_tensor(x[b][:, t, :], h[b, t][:].indirect(idx2[:]), wgt_sb[:], ALU.mult)

        def bound(b, slices, cols):
            nc.scalar.activation(out=y[b][:, slices, cols], in_=x[b][:, slices, cols], func=ACT.Tanh)

        def with_gain(b, cols, rounded):
            width = cols.stop - cols.start
            nc.vector.tensor_tensor(
                rounded.rearrange("p (c i t) -> p c t i", i=4, t=4),
                y[b][:, :, cols].rearrange("p t (c i) -> p c t i", i=4),
                gain_sb[:, b, :].unsqueeze(1).unsqueeze(3).broadcast_to([P, width // 4, 4, 4]),
                ALU.mult,
            )

        first_pass, second_pass, both = slice(0, 1), slice(1, 2), slice(0, 2)
        nc.sync.dma_start(out=tab_plane[96:P, :].bitcast(I32), in_=tab_scales.rearrange("a q t -> (a q) t").bitcast(I32))
        nc.sync.dma_start(idx[:], offs)
        w1_raw[0, 0] = load_w1(0, first_pass)
        for a in range(2):
            tab_sb[a] = staged([P, T], I32, "tab_sb", [0, "big1"][a])
        load_table(0, slice(0, T))
        for q in range(4):
            nc.sync.dma_start(
                out=w1_plane_raw[32 * q : 32 * q + 4, :].bitcast(I32).rearrange("r (a c) -> r a c", a=2),
                in_=w1_scales[:, 4 * q : 4 * q + 4, :].bitcast(I32).rearrange("a r c -> r a c"),
            )
        w1_raw[0, 1] = load_w1(0, second_pass)
        load_table(1, slice(0, 1280))
        for b in range(2):
            w1_sb[b] = kept([P, 2, 2 * W], U8, "w1_sb%d" % b)
            x[b] = kept([P, 4, M], F32, "x%d" % b)
        nc.vector.tensor_copy(v_rows[:], tab_plane[:].indirect(idx[:]))
        place_scale_rows(0)
        load_table(1, slice(1280, T))
        w2_raw[0, 0] = load_rows(w2, 0, slice(0, W), "w2a")
        place_scale_rows(1)
        w2_raw[0, 1] = load_rows(w2, 1, slice(0, W), "w2b")
        w1_raw[1] = load_w1(1, both)
        wgt_sb = kept([P, M], F32, "wgt_sb")
        nc.sync.dma_start(out=wgt_sb[:], in_=wgt)
        nc.sync.dma_start(idx2[:], offs2)
        w2_raw[1, 0] = load_rows(w2, 0, slice(W, 2 * W), "big2")
        w2_raw[1, 1] = load_rows(w2, 1, slice(W, 2 * W), "big3")
        w5_raw[0] = load_rows(w5, 0, every, "w2a")
        gain_sb = kept([P, 2, 4], F32, "gain_sb")
        nc.sync.dma_start(out=gain_sb[:], in_=gain.rearrange("(b p t) -> p b t", b=2, t=4))
        w5_raw[1] = load_rows(w5, 1, every, 8192)
        pr_raw[0] = load_rows(prompts, 0, every, "big1")
        pr_raw[1] = load_rows(prompts, 1, every, "big5")
        w4_sb = kept([P, 2, N], I32, "w4_sb")
        nc.sync.dma_start(out=w4_sb[:], in_=w4_words.rearrange("a p c i -> p a (c i)").bitcast(I32))
        load_scale_rows(w4_plane, 0, w4_scales)
        bias_sb = kept([P, N // P], F32, "bias_sb")
        with nc.allow_non_contiguous_dma(reason="one bias value for each output row"):
            nc.sync.dma_start(out=bias_sb[:], in_=bias.rearrange("(j p) -> p j", p=P))

        order_w1_words(0, first_pass, w1_raw[0, 0])
        gather_words(0, 0)
        order_w1_scales(slice(0, 1), "w1_plane00")
        sweep(0, 0, 0, start=True)
        order_w1_scales(slice(2, 3), "w1_plane10")
        order_w1_scales(slice(1, 4, 2), "w1_plane1")
        order_w1_words(0, second_pass, w1_raw[0, 1])
        gather_words(0, 1, "w1_plane_raw")
        sweep(0, 0, 1, start=True)
        gather_words(1, 0)
        sweep(0, 1, 0)
        gather_words(1, 1)
        sweep(0, 1, 1)
        for a in range(2):
            w2_rounded[0, a] = kept([P, 4 * W], BF16, "r0%d" % a)
        round_w2(w2_rounded[0, 0], w2_raw[0, 0], slice(0, P), [slice(0, 2)], False)
        round_w2(w2_rounded[0, 0], w2_raw[0, 0], slice(0, P), [slice(2, 4)], True)
        quantize_w2(0, 0, range(4))
        for pair, share in enumerate([88, 40]):
            round_w2(w2_rounded[0, 1], w2_raw[0, 1], slice(0, share), [slice(2 * pair, 2 * pair + 2)], False)
            round_w2(w2_rounded[0, 1], w2_raw[0, 1], slice(share, P), [slice(2 * pair, 2 * pair + 2)], True)
        quantize_w2(0, 1, [0])
        quantize_w2(0, 1, [1])
        quantize_w2(0, 1, [2, 3])
        order_w1_words(1, both, w1_raw[1])
        for t in range(4):
            close(0, t, "h0%d" % t)
        for a in range(2):
            for c in range(2):
                sweep(1, a, c, start=(a == 0))
        for t in range(4):
            pick(0, t)
        w2_rounded[1, 0] = staged([P, 4 * W], BF16, "r10", "w2_000")
        round_w2(w2_rounded[1, 0], w2_raw[1, 0], slice(0, P), [slice(0, 4)], True)
        w2_rounded[1, 1] = staged([P, 4 * W], BF16, "r11", "r10")
        round_w2(w2_rounded[1, 1], w2_raw[1, 1], slice(0, P), [slice(0, 4)], False)
        quantize_w2(1, 0, range(4))
        quantize_w2(1, 1, range(4))
        y[0] = kept([P, 4, M], F32, "y0")
        y[1] = staged([P, 4, M], F32, "y1", "big3")
        for pair in range(2):
            bound(0, slice(2 * pair, 2 * pair + 2), every)
        w5_rounded = staged([P, 4 * N], BF16, "rounded", "r00")
        for cols in [slice(0, 352), slice(352, N)]:
            round_into(w5_rounded[:, 4 * cols.start : 4 * cols.stop], w5_raw[0][:, :, cols], cols.start == 0)
        z0_rounded = kept([P, 4 * M], BF16, "z0_rounded")
        with_gain(0, every, z0_rounded[:])
        w5_q[0] = quantize(w5_rounded[:], "w5_0")
        for t in range(4):
            close(1, t, "h1%d" % t)
        for t in range(4):
            pick(1, t)
        w5_rounded = round_plain(w5_raw[1], every, True, "w2_100")
        z0 = quantize(z0_rounded[:], "z0", 8192)
        w5_q[1] = quantize(w5_rounded[:], "w5_1")
        pr_rounded = {}
        pr_rounded[0, 0] = round_plain(pr_raw[0], halves[0], True, "v_words00")
        pr_rounded[1, 0] = round_plain(pr_raw[1], halves[0], False, "pr_rounded10")
        for u in range(2):
            bound(1, slice(0, 4), halves[u])
            pr_rounded[u, 1] = round_plain(pr_raw[u], halves[1], True, "pr_rounded%d1" % u)

        flags = {}

        def add_pass(u, j, codes, plane, rhs, rhs_plane, start=False, stop=False):
            if start:
                flags[u, j] = psum.tile([P, half], F32, name="flags", tag="bank%d" % (4 * u + j))
            nc.tensor.matmul_mx(
                out=flags[u, j][:], lhsT=codes.bitcast(FP8X4), lhsT_scale=plane,
                rhs=rhs.bitcast(FP8X4), rhs_scale=rhs_plane, start=start, stop=stop,
            )

        for u in range(2):
            for j, rows in enumerate(blocks):
                add_pass(u, j, w4_sb[:, 0, rows], w4_plane[:, rows], z0[0][:, halves[u]], z0[1][:, halves[u]], start=True)
        for u, cols in enumerate(halves):
            pr_q[0, u] = quantize(pr_rounded[0, u][:], "pr_0%d" % u)
            z1_rounded = kept([P, 4 * half], BF16, "z1%d_rounded" % u)
            with_gain(1, cols, z1_rounded[:])
            pr_q[1, u] = quantize(pr_rounded[1, u][:], "pr_1%d" % u)
            z1 = quantize(z1_rounded[:], "z1%d" % u)
            for j, rows in enumerate(blocks):
                add_pass(u, j, w5_q[0][0][:, rows], w5_q[0][1][:, rows], pr_q[0, u][0][:], pr_q[0, u][1][:])
            result = kept([P, N // P, half], F32, "result%d" % u)
            for j, rows in enumerate(blocks):
                add_pass(u, j, w5_q[1][0][:, rows], w5_q[1][1][:, rows], pr_q[1, u][0][:], pr_q[1, u][1][:])
                add_pass(u, j, w4_sb[:, 1, rows], w4_plane[4:P, rows], z1[0][:], z1[1][:], stop=True)
                nc.scalar.activation(out=result[:, j, :], in_=flags[u, j][:], func=ACT.Abs, bias=bias_sb[:, j : j + 1])
                nc.sync.dma_start(out=out[rows, cols], in_=result[:, j, :])
